import numpy as np, ml_dtypes
CORES = [8,9,10,11,12,13]
N = 6
BF = ml_dtypes.bfloat16
def gentries(a):
    return np.ascontiguousarray(a.reshape(8, 16, -1).transpose(0, 2, 1)).reshape(8, -1)
def gtable(e):
    e = np.asarray(e); return np.ascontiguousarray(e.reshape(8, -1, 16).transpose(0, 2, 1)).reshape(128, -1).astype(np.int32)
V, SH, L, RO, WT = 1536, 2, 256, 4, 2
R = V << SH
NC = 8
def near(rng, X, x):
    return np.clip(np.take_along_axis(X, x[:, :, None, :], 3) + rng.integers(-1, 2, (N, 8, 16, L)), 0, 15)
def scene(rng, strong):
    M = V // NC
    lab = rng.permuted(np.tile(np.arange(V) % NC, (8, 1)), axis=1); order = np.argsort(lab, axis=1, kind="stable")
    if strong: cen = np.tile(2 + 11 * (np.arange(NC) % 2), (8, 16, 1)); w = 1
    else: cen = rng.integers(2, 14, (8, 16, NC)); w = 3
    X = np.clip(np.take_along_axis(cen, np.repeat(lab, 2 ** SH, axis=1)[:, None, :], 2)[None] + rng.integers(-w, w + 1, (N, 8, 16, R)), 0, 15)
    to = np.where(rng.random((N, 8, 16, V)) < 0.4, rng.integers(0, NC, (N, 8, 16, V)), lab[None, :, None, :])
    gene = order[np.arange(8)[None, :, None, None], to * M + rng.integers(0, M, (N, 8, 16, V))]
    P = gene * 2 ** SH + rng.integers(0, 2 ** SH, (N, 8, 16, V))
    x = rng.integers(0, R, (N, 8, L)); th = rng.integers(0, 21, (N, 8, 16, RO))
    return lab, X, P, x, near(rng, X, x), th
def pack(X, P, x, z, th):
    return {"prof": X.reshape(N, 128, R).astype(np.float32).astype(BF), "par": np.ascontiguousarray(P.reshape(N, 128, V)).astype(np.int32),
            "rec": np.stack([gtable(a) for a in x]), "zf": z.reshape(N, 128, L).astype(np.float32).astype(BF), "th": np.ascontiguousarray(th.reshape(N, 128, RO)).astype(np.int32)}
def setup_inputs(rng):
    lab, X, P, x, z, th = scene(rng, False)
    return pack(X, P, x, z, th)
def setup_inputs_spread(rng):
    X = (rng.random((N, 8, 16, R)) * 2.0 ** rng.integers(0, 5, (N, 8, 1, R))).astype(np.int64)
    P = (R * rng.random((N, 8, 16, V)) ** rng.choice(np.array([1, 1, 3]), (N, 8, 1, V))).astype(np.int64)
    x = (R * rng.random((N, 8, L)) ** rng.choice(np.array([1, 2, 4]), (N, 8, 1))).astype(np.int64)
    z = (rng.random((N, 8, 16, L)) * 2.0 ** rng.integers(0, 5, (N, 8, 1, L))).astype(np.int64)
    th = (64 * rng.random((N, 8, 16, RO)) ** 5).astype(np.int64)
    return pack(np.minimum(X, 15), np.minimum(P, R - 1), np.minimum(x, R - 1), np.minimum(z, 15), np.minimum(th, 63))
def setup_inputs_ends(rng):
    f = rng.integers(0, 2, 8); cls = rng.integers(0, 2, (8, V)); cls[:, 0] = f; cls[:, V - 1] = 1 - f
    cr = np.repeat(cls, 2 ** SH, axis=1); pure = rng.random((8, R)) < 0.75; pure[:, 0] = True; pure[:, R - 1] = True
    X = np.where(pure[None, :, None, :], 15 * cr[None, :, None, :], 15 * rng.integers(0, 2, (N, 8, 16, R)))
    own = np.where(cls == f[:, None], 0, R - 1)[None, :, None, :]; e = rng.random((N, 8, 16, V))
    P = np.where(e < 0.45, own, np.where(e < 0.65, R - 1 - own, rng.integers(0, R, (N, 8, 16, V))))
    e = rng.random((N, 8, L)); x = np.where(e < 0.35, 0, np.where(e < 0.7, R - 1, rng.integers(0, R, (N, 8, L))))
    x[:, :, 0] = 0; x[:, :, 1] = R - 1; x[:, :, L - 2] = R - 1; x[:, :, L - 1] = 0
    c = cr[np.arange(8)[None, :, None], x]; like = rng.random((N, 8, L)) < 0.8; like[:, :, :2] = True; like[:, :, L - 2:] = True
    z = np.where(like[:, :, None, :], 15 * c[:, :, None, :], 15 * rng.integers(0, 2, (N, 8, 16, L)))
    th = 63 * rng.integers(0, 2, (N, 8, 16, RO)); turn = rng.integers(0, 2, (N, 8)); turn[N - 1, 7] = 0
    for g in range(8):
        lo = np.flatnonzero(pure[g] & (cr[g] == f[g])); hi = np.flatnonzero(pure[g] & (cr[g] != f[g]))
        for q in range(N):
            a = np.where(rng.random(16) < 0.5, 0, rng.choice(lo, 16)); b = np.where(rng.random(16) < 0.5, R - 1, rng.choice(hi, 16))
            a[:2] = R - 1
            if turn[q, g]: b[15] = 0; b[1] = 0
            P[q, g, :, 0] = a; P[q, g, :, V - 1] = b
    return pack(X, P, x, z, th)
def level(rng, m):
    sh = rng.integers(0, 16, m.shape)
    return (m >> 4)[None] + (((np.arange(16)[:, None] + sh[None]) & 15) < (m & 15)[None])
def setup_inputs_corners(rng):
    lab, X, P, x, z, th = scene(rng, False)
    th[..., 0] = rng.choice(np.array([0, 0, 1, 5, 20, 63]), (N, 8, 16)); k = np.arange(16)[:, None]; l = np.arange(L)
    half = (l & 7) == 3; farx = (l & 7) == 5; fary = (l & 7) == 6; few = farx | fary; hl = np.flatnonzero(half)
    for q in range(N):
        for g in range(8):
            o = 1 + rng.permutation(V - 2); u, v, w = np.array(o[:L]), o[L:2 * L], o[2 * L:3 * L]; u[0] = 0; u[L - 1] = V - 1
            pool = rng.permutation(((o[3 * L:] << SH)[:, None] + np.arange(2 ** SH)[None]).reshape(-1))[:482]
            xr, yr, br = [(a << SH) + rng.integers(0, 2 ** SH, L) for a in (u, v, w)]; xr[0] = 0; xr[L - 1] = R - 1
            flip = rng.integers(0, 2, L); beta = rng.integers(80, 240, L); beta[hl] = 240; bm = np.where(flip == 1, 240 - beta, beta)
            X[q, g][:, pool] = level(rng, np.arange(482) % 241); X[q, g][:, yr] = (15 * (1 - flip))[None]; X[q, g][:, br] = level(rng, bm)
            rho = xr & 15; key = rng.random((16, L)); key[rho, l] = 2.0; place = np.argsort(np.argsort(key, axis=0), axis=0)
            nw = np.where(half | few, 15, rng.choice(np.array([0, WT - 1, WT, WT, WT + 1, 15]), L))
            twin = (nw == WT - 1) & (rng.random(L) < 0.25)
            X[q, g][:, yr[twin] ^ 1] = (15 * (1 - flip[twin]))[None]; th[q, g, rho[twin], 0] = 0
            e = np.where(place < nw[None], rng.choice(np.array([0, 0, 1, 5]), (16, L)), -1)
            m = beta[None] - th[q, g, :, :1] - e
            A = pool[np.where(flip[None] == 1, 240 - m, m)]
            odd = (rng.integers(0, 2, L) == 1) & ~(half | few)
            B = np.where(odd[None] & ((k & 1) == 1), pool[241 + bm][None], br[None])
            B[rho[twin], l[twin]] = yr[twin] ^ 1
            A = np.where((place == 14) & (nw[None] < 15), B, A); A[rho, l] = yr
            lo = np.where(rho == 0, 1, 0)[hl]; hi = np.where(rho == 15, 14, 15)[hl]
            A[lo, hl] = pool[np.where(flip[hl] == 1, 239, 1)]; A[hi, hl] = pool[240 * flip[hl]]; B[lo, hl] = pool[241 + bm[hl]]
            mode = rng.integers(0, 5, L)[None]; some = rng.choice(pool, (16, L))
            C = np.where(mode == 0, yr[None], np.where(mode == 1, xr[None], np.where(mode == 2, np.where(k == 15, some, yr[None]), np.where(mode == 3, np.where(rng.random((16, L)) < 0.5, yr[None], xr[None]), some))))
            far = pool[240 * np.where(farx, flip, 1 - flip)[None] + 241 * rng.integers(0, 2, (16, L))]; far[0] = np.where(farx, xr, yr)
            C = np.where(few[None], far, C)
            P[q, g][:, u] = A; P[q, g][:, v] = B; P[q, g][:, w] = C
            x[q, g] = xr; z[q, g] = (15 * flip)[None]
    return pack(X, P, x, z, th)
def setup_inputs_crowd(rng):
    lab, X, P, x, z, th = scene(rng, True); th = rng.integers(0, 64, th.shape)
    for q in range(N):
        for g in range(8):
            c = int(rng.integers(0, 2)); a = rng.permutation(np.flatnonzero((lab[g] & 1) == c)); b = rng.permutation(np.flatnonzero((lab[g] & 1) != c))
            x0 = (a[:4] << SH) + rng.integers(0, 2 ** SH, 4); y0 = (b[:4] << SH) + rng.integers(0, 2 ** SH, 4)
            for i in range(4):
                P[q, g, :, a[i]] = (rng.choice(a, 16) << SH) + rng.integers(0, 2 ** SH, 16)
                P[q, g, ((a[i] << SH) + np.arange(2 ** SH)) & 15, a[i]] = y0[i]
                P[q, g, :, b[i]] = (rng.choice(b, 16) << SH) + rng.integers(0, 2 ** SH, 16)
            mode = (g + q) % 3
            if mode == 0: x[q, g] = x0[0]
            elif mode == 1: x[q, g] = x0[rng.integers(0, 4, L)]
            else: x[q, g] = (a[0] << SH) + rng.integers(0, 2 ** SH, L)
            if q % 4 == 1 and g % 2 == 1:
                r = (a[4] << SH) + int(rng.integers(0, 2 ** SH)); P[q, g, :, a[4]] = r; x[q, g, int(rng.integers(0, L))] = r
    z = near(rng, X, x)
    for q in range(3, N, 4):
        away = rng.random((8, L)) < 0.5; away[:, 0] = True; away[:, L - 1] = False
        z[q] = np.where(away[:, None, :], 15 - z[q], z[q])
    return pack(X, P, x, z, th)
def setup_inputs_counts(rng):
    cls = rng.permuted(np.tile(np.arange(V) & 1, (8, 1)), axis=1); order = np.argsort(cls, axis=1, kind="stable")
    X = 6 + 2 * np.repeat(cls, 2 ** SH, axis=1)[None, :, None, :] + rng.integers(0, 2, (N, 8, 16, R))
    off = ((np.arange(16)[:, None] - (np.arange(V) << SH)[None]) & 15) < 2 ** SH + 2
    to = np.where(off[None, None], 1 - cls[None, :, None, :], cls[None, :, None, :])
    gene = order[np.arange(8)[None, :, None, None], to * (V // 2) + rng.integers(0, V // 2, (N, 8, 16, V))]
    P = gene * 2 ** SH + rng.integers(0, 2 ** SH, (N, 8, 16, V))
    x = rng.integers(0, R - 2 ** SH, (N, 8, L))
    for q in range(1, N, 2):
        g = int(rng.integers(0, 8)); r = ((V - 1) << SH) + int(rng.integers(0, 2 ** SH))
        P[q, g, :, V - 1] = r; x[q, g, int(rng.integers(0, L))] = r
    z = 6 + 2 * cls[np.arange(8)[None, :, None], x >> SH][:, :, None, :] + rng.integers(0, 2, (N, 8, 16, L))
    lev = 4 + 4 * rng.permuted(np.tile(np.arange(8), (N, RO, 1)), axis=2)
    th = lev.transpose(0, 2, 1)[:, :, None, :] + rng.integers(0, 4, (N, 8, 16, RO))
    th[..., 0] = 0; th[1::4, :, :, 1] = 63; th[2::4, :, :, 2] = 63; th[3::4, :, :, 2] = 63
    for q in range(1, N, 4):
        g = int(rng.integers(0, 8)); X[q, g] = 6 + rng.integers(0, 4, (16, 1))
        th[q, g, :, 2] = 63; th[q, g, rng.permutation(16)[:WT], 2] = 0
    return pack(X, P, x, z, th)
def check_inputs(d):
    bad = []
    for k, lo, hi in (("prof", 0, 15), ("par", 0, R - 1), ("rec", 0, R - 1), ("zf", 0, 15), ("th", 0, 63)):
        a = np.asarray(d[k]).astype(np.float64)
        if not (np.min(a) >= lo and np.max(a) <= hi): bad.append("range of " + k)
        elif np.any(a != np.floor(a)): bad.append("whole numbers in " + k)
    return bad
def look(tab, n):
    return np.take_along_axis(tab, n[:, None, :], 2)
def row_of(tile, k):
    return np.take_along_axis(tile, k[:, None, :], 1)[:, 0]
def dist(w, p):
    return np.add.reduce(np.abs(w - p[:, :, None, :]), axis=1)
def reference(prof, par, rec, zf, th):
    X = prof.astype(np.float32).astype(np.int32).reshape(N, 8, 16, R); P = par.astype(np.int64).reshape(N, 8, 16, V)
    x = np.stack([gentries(a) for a in rec]).astype(np.int64); z = zf.astype(np.float32).astype(np.int32).reshape(N, 8, 16, L)
    tt = th.astype(np.int64).reshape(N, 8, 16, RO); breaks = [0] * N; rows = np.arange(16)[None, :, None]
    for t in range(RO):
        for q in range(N):
            h = (q - t) % N; xs, zs = x[h], z[h]
            A = look(P[q], xs >> SH); rho = (xs + t) & 15; y = row_of(A, rho); B = look(P[q], y >> SH); Xy = look(X[q], y)
            wa = look(X[q], A.reshape(8, -1)).reshape(8, 16, 16, L); wb = look(X[q], B.reshape(8, -1)).reshape(8, 16, 16, L)
            e1 = dist(wb, zs) - dist(wa, zs); e2 = dist(wa, Xy) - dist(wb, Xy)
            s = tt[q, :, :, t][:, :, None] + (breaks[q] & 15)
            wit = (rows != rho[:, None, :]) & (A != B) & (e1 >= s) & (e2 >= s)
            broken = np.count_nonzero(wit, axis=1) >= WT
            kb = np.argmax(np.where(wit, e1 + e2, -1), axis=1)
            C = look(P[q], row_of(B, kb) >> SH); wc = look(X[q], C.reshape(8, -1)).reshape(8, 16, 16, L)
            y1 = row_of(C, np.argmin(np.where(C == y[:, None, :], 1000, dist(wc, zs)), axis=1))
            x1 = row_of(C, np.argmin(np.where(C == xs[:, None, :], 1000, dist(wc, Xy)), axis=1))
            for g in range(8):
                b = np.flatnonzero(broken[g])
                for a, new in ((xs, y1), (y, x1)):
                    u, i = np.unique(a[g, b] >> SH, return_index=True); P[q, g, rho[g, b[i]], u] = new[g, b[i]]
            breaks[q] = int(np.count_nonzero(broken))
            z[h] = np.where(broken[:, None, :], (zs + look(X[q], y1)) >> 1, zs); x[h] = np.where(broken, y1, y)
    return {"ypar": P.reshape(N, 128, V).astype(np.float32), "yrec": np.stack([gtable(a) for a in x]).astype(np.float32), "yz": z.reshape(N, 128, L).astype(np.float32).astype(BF)}

@@ -1,0 +1,739 @@
+from concourse.mybir import AluOpType, AxisListType, ActivationFunctionType
+
+ALU, AF = AluOpType, ActivationFunctionType
+
+NV, NR, NL, RO = 1536, 6144, 256, 4
+F, B, I, U = "float32", "bfloat16", "int32", "uint16"
+SB = {
+    "tab": (F, 2048), "pari": (I, NV), "prf": (B, NR + NL * RO), "reci": (I, 16), "thi": (I, 4), "thf": (F, 4),
+    "zfin": (B, NL), "xfin": (F, 16),
+    "ia": (I, 16), "ib": (I, 16), "ct": (I, 16), "o16": (U, 16), "o8": (U, 8), "pcol": (F, 1), "rrow": (F, 256),
+    "onef": (F, 128), "idf": (F, 128), "idb": (B, 256), "nid": (B, 128), "bigp": (B, 128), "bign": (B, 128), "oneb": (B, 128),
+    "indf": (F, 8), "ind16": (F, 8), "bof": (F, 128), "bo17": (B, 128), "cntw": (F, 128), "d256": (B, 256), "dpen": (B, 256),
+    "rsmax": (B, 256), "rsmin": (B, 256), "rsmul": (B, 128), "sr": (B, 384), "cr4": (B, 256), "chi": (B, 16),
+    "rh": (B, 512), "pw": (F, 128), "tmpa": (F, 128), "tmpb": (F, 128), "c1": (F, 1), "c2": (F, 1), "rw": (F, 128), "thm": (F, 256),
+    "r8": (F, 128), "bov": (B, 384), "zt": (B, 256), "pt": (B, 256), "dhi": (B, 16), "dlo": (B, 8), "lc": (F, 64),
+    "xg16": (U, 16), "ri": (I, 16), "ri2": (I, 16), "rho16": (U, 16), "gf": (F, 32), "kr": (U, 512), "x0": (F, 256),
+    "mask": (B, 256), "notm": (B, 256), "af": (F, 256), "bf": (F, 256), "cf": (F, 256), "a16": (U, 256), "b16": (U, 256), "c16": (U, 256),
+    "ma": (F, 256), "anm": (F, 256), "ys": (F, 256), "y16": (U, 16), "yg16": (U, 16), "pp": (B, 256), "eab": (B, 256),
+    "wa": (B, 4096), "wb": (B, 4096), "wc": (B, 4096),
+    "mza": (B, 4096), "mpa": (B, 4096), "mzb": (B, 4096), "mpb": (B, 4096), "mzc": (B, 4096), "mpc": (B, 4096),
+    "eq": (B, 8192), "vio": (B, 512), "sg": (B, 256), "ks": (F, 256), "cs": (B, 256), "nbp": (B, 32), "kk": (F, 16), "kx": (F, 256),
+    "brm": (F, 16), "ki": (I, 16), "kg": (I, 16), "cg16": (U, 16), "fb": (F, 32), "eqy": (B, 256), "eqx": (B, 256),
+    "rb": (B, 192), "tot": (F, 32), "lose": (B, 512), "off": (F, 32), "off16": (U, 32), "zc": (F, 16),
+    "ss": (F, 512), "vi": (I, 32), "vj": (I, 32), "vf": (F, 32), "ex": (F, 512), "mm": (F, 512), "rg": (F, 256), "xs": (F, 256),
+    "zo": (F, 16), "zo16": (U, 16), "zs": (B, 256), "zh": (B, 256), "cn": (F, 1), "cni": (I, 1), "cnj": (I, 1), "scol": (F, 1),
+}
+for _t in range(RO):
+    SB["xl%d" % _t] = (F, 16)
+    SB["sxl%d" % _t] = (F, 16)
+    SB["sz%d" % _t] = (B, NL)
+    if _t:
+        SB["xr%d" % _t] = (F, NL)
+        SB["sxr%d" % _t] = (F, NL)
+SCRATCH, AT, _fill = {}, {}, {}
+for _k, (_d, _n) in SB.items():
+    if _n > 32:
+        SCRATCH[_k], AT[_k] = ("sbuf", [128, _n], _d), (_k, 0)
+    else:
+        AT[_k] = ("few" + _d, _fill.get(_d, 0))
+        _fill[_d] = _fill.get(_d, 0) + (_n + 15) // 16 * 16
+for _d, _n in _fill.items():
+    SCRATCH["few" + _d] = ("sbuf", [128, _n], _d)
+PSB = False
+for _b in range(8):
+    SCRATCH["pb%d" % _b] = ("psum", [128, 1024], B) if PSB and _b < 2 else ("psum", [128, 512], F)
+SEMAPHORES = (["qv", "qa", "qp", "qg", "sent", "st0", "st1", "st2", "st3"] + ["ld%d" % i for i in range(6)]
+              + ["ar%d%s" % (t, w) for t in range(1, RO) for w in "lmrzy"] + ["ar4l", "ar4z"])
+
+ABS = {('a', 'p', 0): 3, ('a', 'z', 0): 1, ('b', 'p', 0): 1, ('b', 'z', 1): 2, ('c', 'p', 0): 2, ('c', 'p', 1): 3}
+WV = {('a', 1)}
+FINE = {('a', 0), ('a', 1)}
+GC, SC, CY, PC, HOP, SELF, WIRE = 1.56, 3.8, 1.0, 0.5, 120.0, 60.0, 2500.0
+TT2 = 0.5 if PSB else 1.0
+STEPS = "a0 b0 a1 b1 k0 p0 k1 c0 p1 c1 e0 e1 l0 l1 n0 n1 z0 z1".split()
+CUT = 64
+BIAS = {'svkr': 7700, 'svys': -3300, 'sapp': -2000, 'sabf': -3000, 'svcn': -5300, 'c0awc': 7700, 'svsr': -600, 'z1gsxl': -2700, 'z1gsz': -3000, 'z1ppb': -3000, 'z1vmm': -3000, 'z1vss': -3000, 'z1vtab': 5000, 'z1vvf': -4000, 'z1vvi': -2000, 'z1vvj': -3000, 'z1vxs': -6000, 'z1vzo': -3000, 'z1xprf': -3000, 'z1xxl': -3000, 'b0awb': -8000, 'svma': -1300, 'z0asxl': 3000, 'sanotm': 1000, 'p0vcs': -1000, 'saaf': -1000, 'c1awc': 3000, 'n1vmzc': -1000,
+        'sveab': -300, 'z0vss': -8000, 'svtab': -1000, 'p1avio': 300, 'p0ppb': 3000, 'p1vks': 1000, 'svcnj': -1000, 'z1asxr': 300, 'svxg': -1000, 'e0veq': -1000, 'n0vmzc': 3000, 'p1vfb': 3000, 'p1vcs': 1000, 'k0vmpa': 3000, 'k0vmpb': 3000, 'k0vmzb': 3000}
+PASSES, INLINE, GREEDY, AHEAD = 1, False, True, 0.35
+ORDER = {}
+K16, BIG = 65536.0, float(2 ** 26)
+
+
+def build(g, T, rank, topo):
+    ops, pre, rhs_at = [], [], {}
+    cur, made, stage = [ops], set(), ["s"]
+    V, A, P = g.vector, g.scalar, g.tensor
+
+    def S(name, lo=0, hi=None, step=1, p=None):
+        if hi is None:
+            hi = 512 if name[:2] == "pb" else SB[name][1]
+        rows = slice(None) if p is None else slice(p, p + 1)
+        n = len(range(lo, hi, step))
+        buf, at = AT.get(name, (name, 0))
+        ap = T[buf][rows, at + lo:at + hi] if step == 1 else T[buf][rows, at + lo:at + hi:step]
+        return (ap, (name, lo, lo + (n - 1) * step + 1), n)
+
+    def two(x):
+        if x[1][0][:2] == "pb":
+            return PSB and x[1][0] in ("pb0", "pb1")
+        return SB[x[1][0]][0] in (B, U)
+
+    def row(r, e):
+        return 8 * e + r
+
+    def W(c, l0, l1, r=None, k=None):
+        a, st = (0, 1) if r is None and k is None else (r, 8) if k is None else (k, 16)
+        return S("w" + c, 16 * l0 + a, 16 * l1, st)
+
+    def op(eng, cost, fn, rd, wr, **kw):
+        d = {"e": eng, "c": cost, "f": fn, "r": [x[1] for x in rd], "w": [x[1] for x in wr]}
+        d["tag"] = stage[0] + eng + (wr + rd)[0][1][0].rstrip("0123456789")
+        d.update(kw)
+        cur[0].append(d)
+        return d
+
+    def gat(win, off):
+        return (win[0].indirect(off[0]), win[1], off[2] * 16, off)
+
+    def rds(*xs):
+        out = []
+        for x in xs:
+            if isinstance(x, tuple):
+                out.append(x)
+                if len(x) == 4:
+                    out.append(x[3])
+        return out
+
+    def vcost(o, xs, rate):
+        if len(o) == 4:
+            return 50 + SC * o[2] * CY
+        if len(xs[0]) == 4:
+            return 50 + GC * o[2] * CY
+        return max(64, rate * xs[0][2]) * CY
+
+    def val(s):
+        return s[0] if isinstance(s, tuple) else s
+
+    def cp(o, x):
+        op("v", vcost(o, [x], 0.5 if two(o) and two(x) else 1), lambda: V.tensor_copy(o[0], x[0]), rds(x), [o])
+
+    def tt(o, x, y, a):
+        r = 1 if "pb" in (x[1][0][:2], y[1][0][:2]) else 2
+        if two(o) and two(x) and two(y):
+            r *= TT2
+        op("v", vcost(o, [x], r), lambda: V.tensor_tensor(o[0], x[0], y[0], a), rds(x, y) + rds(o)[1:], [o])
+
+    def ts(o, x, s1, a, s2=None, b=None):
+        c = vcost(o, [x], 0.5 if two(o) and two(x) else 1)
+        if b is None:
+            op("v", c, lambda: V.tensor_scalar(o[0], x[0], val(s1), None, a), rds(x, s1), [o])
+        else:
+            op("v", c, lambda: V.tensor_scalar(o[0], x[0], val(s1), val(s2), a, b), rds(x, s1, s2), [o])
+
+    def scan(o, d0, d1, init, a, b):
+        c = max(64, (0.5 if two(o) and two(d0) and two(d1) else 1) * o[2]) * CY
+        op("v", c, lambda: V.tensor_tensor_scan(o[0], d0[0], d1[0], init, a, b), [d0, d1], [o])
+
+    def red(o, x):
+        op("v", max(64, x[2]) * CY, lambda: V.tensor_reduce(o[0], x[0], AxisListType.X, ALU.add), [x], [o])
+
+    def ms(o, c):
+        op("v", max(64, o[2] * (0.5 if two(o) else 1)) * CY, lambda: V.memset(o[0], c), [], [o])
+
+    def act(o, x, f, bias=0.0, scale=1.0):
+        c = 65 + GC * o[2] * CY if len(x) == 4 else max(64, o[2]) * CY
+        op("a", c, lambda: A.activation(o[0], x[0], f, bias=bias, scale=scale), rds(x), [o])
+
+    def mm(o, l, r, start=False, stop=False):
+        c = max(64, r[2]) * (1 if two(r) else 4) * PC
+        op("p", c, lambda: P.matmul(o[0], l[0], r[0], start, stop), [l, r], [o], start=start, stop=stop)
+
+    def tr(o, x):
+        op("p", 128 * PC, lambda: P.transpose(o[0], x[0], S("idb", 0, 128)[0]), [x, S("idb", 0, 128)], [o], start=True, stop=True)
+
+    def twice(bank, src, tb):
+        if not PSB:
+            for h in range(2):
+                for e in range(2):
+                    mm(S(bank, 256 * h + e, 256 * h + 256, 2), S("idb", 0, 128), src(128 * h, 128 * h + 128), True, True)
+            return
+        for h in range(2):
+            tr(S(bank, 512 + 128 * h, 640 + 128 * h), src(128 * h, 128 * h + 128))
+        act(S(tb), S(bank, 512, 768), AF.Copy)
+        for h in range(2):
+            for e in range(2):
+                tr(S(bank, 256 * h + e, 256 * h + 256, 2), S(tb, 128 * h, 128 * h + 128))
+
+    def part(n):
+        if n == 8:
+            return S("bo17")
+        o = S("bov", 64 * n - 128, 64 * n)
+        if ("part", n) not in made:
+            made.add(("part", n))
+            keep, cur[0] = cur[0], pre
+            ts(S("tmpa"), S("r8"), n - 0.5, ALU.is_lt, -float(2 ** 17), ALU.mult)
+            tt(o, S("tmpa"), S("bof"), ALU.mult)
+            cur[0] = keep
+        return o
+
+    def iota(o, pat, base, cm):
+        if SB[o[1][0]][0] == I:
+            fn = lambda: g.iota(o[0], pat, base, cm)
+        else:
+            fn = lambda: g.iota(o[0], pat, base, cm, allow_small_or_imprecise_dtypes=True)
+        op("g", 130 + 2 * o[2] * CY, fn, [], [o])
+
+    def sel(o, x, pat, cmp, base, cm):
+        op("g", 170 + 2 * o[2] * CY, lambda: g.affine_select(o[0], x[0], pat, cmp, 0.0, base, cm), [x], [o])
+
+    def dma(q, sem, dst, src, rd, wr, lat):
+        e = g.sync if q == "s" else g.scalar
+        op(q, 60, lambda: e.dma_start(dst, src), rd, wr, sem=sem, n=16, lat=lat)
+
+    def send(src, dst, to, sem, model):
+        me, core = T.cores[rank], T.cores[to]
+        rid, pid = topo.addr(core)[:2]
+        eng = topo.engines(me, core)[::2]
+        d = op("g", 200, lambda: g.remote_dma(dst[0], src[0], T.sem[sem], T.sem["sent"], pid, rid, sum(1 << e for e in eng)),
+               [src], [], send=len(eng))
+        op("x", 0, None, [], [dst], sem=sem, n=len(eng), after=d, lat=model)
+
+    def rhs(*co):
+        if co not in rhs_at:
+            at = sum(len(c) for c in rhs_at) * 8
+            rhs_at[co] = at
+            keep, cur[0] = cur[0], pre
+            for i, c in enumerate(co):
+                if c:
+                    ts(S("rh", at + 8 * i, at + 8 * i + 8), S("indf"), float(c), ALU.mult)
+            cur[0] = keep
+        return S("rh", rhs_at[co], rhs_at[co] + 8 * len(co))
+
+    def acc(bank, k, l, co):
+        nz = [i for i, c in enumerate(co) if c]
+        if nz:
+            a, b = nz[0], nz[-1] + 1
+            mm(S(bank, 128 * a + k, 128 * b, 16), l, rhs(*co[a:b]))
+
+    cur[0] = pre
+    dma("s", "ld0", S("reci")[0], T.rec[:], [], [S("reci")], 2000)
+    dma("s", "ld1", T.pari[:], T.par[:], [], [S("pari")], 4500)
+    dma("a", "ld2", S("thi")[0], T.th[:], [], [S("thi")], 2000)
+    dma("a", "ld3", T.prf[:, NR:NR + NL], T.zf[:], [], [S("prf", NR, NR + NL)], 2200)
+    dma("s", "ld4", T.prf[:, 0:NR // 2], T.prof[:, 0:NR // 2], [], [S("prf", 0, NR // 2)], 8000)
+    dma("a", "ld5", T.prf[:, NR // 2:NR], T.prof[:, NR // 2:NR], [], [S("prf", NR // 2, NR)], 8000)
+    ms(S("onef"), 1.0)
+    iota(S("ia"), [[0, 16]], 0, 1)
+    iota(S("ib"), [[1, 16]], 0, 0)
+    iota(S("rrow"), [[0, 16], [1, 16]], 0, 0)
+    iota(S("r8"), [[0, 16], [1, 8]], 0, 0)
+    sel(S("idf"), S("onef"), [[-1, 128]], ALU.is_equal, 0, 1)
+    sel(S("tmpa"), S("onef"), [[-16, 8], [0, 16]], ALU.is_ge, 0, 1)
+    sel(S("bof"), S("tmpa"), [[16, 8], [0, 16]], ALU.is_ge, 15, -1)
+    for j in range(32):
+        if j % 8:
+            lo = 256 * j + 128 * (j % 16 // 8)
+            iota(S("eq", lo, lo + 16 * (j % 8)), [[0, 16 * (j % 8)]], 0, 0)
+    ts(S("ri"), S("ia"), 15, ALU.bitwise_and)
+    cp(S("pcol"), S("ri", 0, 1))
+    cp(S("o16"), S("ib"))
+    ts(S("ct"), S("ib"), 16.0, ALU.mult, S("pcol"), ALU.add)
+    ts(S("ri2"), S("ct"), 63, ALU.bitwise_and, 3, ALU.arith_shift_right)
+    cp(S("o8"), S("ri2", 0, 8))
+    for t in range(RO):
+        ts(S("lc", 16 * t, 16 * t + 16), S("ct"), float(NR + NL * t), ALU.add)
+    ts(S("d256"), S("rrow"), S("pcol"), ALU.is_equal)
+    ts(S("dpen"), S("d256"), -1.0, ALU.add, 16384.0, ALU.mult)
+    ts(S("rsmax"), S("rrow"), 0.0, ALU.is_equal, -float(2 ** 60), ALU.mult)
+    ts(S("rsmin"), S("rrow"), 0.0, ALU.is_equal, float(2 ** 60), ALU.mult)
+    ts(S("rsmul"), S("rrow", 0, 128), 0.0, ALU.not_equal)
+    cp(S("idb", 0, 128), S("idf"))
+    cp(S("idb", 128, 256), S("idf"))
+    ts(S("nid"), S("idf"), -1.0, ALU.mult)
+    ts(S("bigp"), S("idf"), BIG, ALU.mult)
+    ts(S("bign"), S("idf"), -BIG, ALU.mult)
+    ms(S("oneb"), 1.0)
+    ms(S("cntw"), -1.0 / 8192)
+    cp(S("indf"), S("bof", 0, 128, 16))
+    ts(S("ind16"), S("indf"), 1.0 / 16, ALU.mult)
+    ts(S("bo17"), S("bof"), -float(2 ** 17), ALU.mult)
+    ms(S("sr", 256, 384), 0.0)
+    ts(S("sr", 256, 384, p=0), S("rrow", 0, 128, p=0), -8192.0, ALU.mult, 15 * 8192.0, ALU.add)
+    ms(S("sr", 256, 384, p=32), -float(2 ** 24))
+    ms(S("cr4"), 0.0)
+    ts(S("cr4", p=0), S("rrow", p=0), 8192.0, ALU.mult)
+    ms(S("cr4", p=32), -121.0 * 2 ** 17)
+    ms(S("chi"), 0.0)
+    ms(S("chi", p=0), 1920.0 * 8192)
+    ms(S("rh"), 0.0)
+    ms(S("nbp"), 0.0)
+    ms(S("tab", NV, 2048), 0.0)
+    ts(S("pw"), S("onef"), 0.5, ALU.mult)
+    ms(S("tmpb"), 0.0)
+    scan(S("tmpa"), S("pw"), S("tmpb"), float(2 ** 21), ALU.mult, ALU.add)
+    tt(S("pw", 0, 16), S("tmpa", 0, 16), S("d256", 0, 16), ALU.mult)
+    red(S("c1"), S("pw", 0, 16))
+    for j in range(8):
+        ts(S("rw", 8 * j, 8 * j + 8), S("indf"), S("c1"), ALU.mult, -(2.0 ** (-16 * j - 13)), ALU.mult)
+        ts(S("rw", 64 + 8 * j, 72 + 8 * j), S("indf"), -256.0, ALU.mult)
+    tt(S("tmpb"), S("tmpa"), S("idf"), ALU.mult)
+    red(S("c2"), S("tmpb"))
+    ts(S("tmpa"), S("d256", 0, 128), S("c2"), ALU.mult, 2.0, ALU.mult)
+    ts(S("tmpb"), S("dpen", 0, 128), -float(2 ** 26), ALU.mult)
+    tt(S("thm", 0, 128), S("tmpa"), S("tmpb"), ALU.max)
+    cp(S("thm", 128, 256), S("thm", 0, 128))
+    ts(S("dlo"), S("indf"), S("pcol"), ALU.mult)
+    ts(S("c1"), S("ia", 0, 1), S("pcol"), ALU.subtract, float(NV), ALU.add)
+    ts(S("dhi", 0, 8), S("indf"), S("c1"), ALU.mult)
+    ts(S("c2"), S("c1"), 128.0, ALU.add)
+    ts(S("dhi", 8, 16), S("indf"), S("c2"), ALU.mult)
+    cp(S("xl0"), S("reci"))
+    cp(S("thf"), S("thi"))
+    cp(S("tab", 0, NV), S("pari"))
+    cur[0] = ops
+
+    tab, prof = S("tab"), S("prf", 0, NR)
+    co = {("a", "z"): (-1, 0, -K16), ("b", "z"): (1, 0, K16), ("a", "p"): (0, 1, K16), ("b", "p"): (0, -1, -K16),
+          ("c", "z"): (2 * K16, 0), ("c", "p"): (0, 2 * K16)}
+
+    def H(name, h, n=128, at=0):
+        return S(name, at + n * h, at + n * h + n)
+
+    def is_abs(c, d, h, k):
+        return k % 8 >= 8 - 2 * ABS.get((c, d, h), 0)
+
+    for t in range(RO):
+        z0 = NR + NL * t
+        xl = "xl%d" % t
+        side = {"z": lambda h, z0=z0: S("prf", z0 + 128 * h, z0 + 128 * h + 128), "p": lambda h: H("pp", h)}
+        dup = {"z": "pb0", "p": "pb1"}
+        flip = [0]
+
+        def wgather(c, h):
+            for l in range(128 * h, 128 * h + 128, CUT):
+                src = gat(prof, S(c + "16", l, l + CUT))
+                if (c, l // 64) in WV:
+                    cp(W(c, l, l + CUT), src)
+                else:
+                    act(W(c, l, l + CUT), src, AF.Copy)
+
+        def dist(c, d, h):
+            m, bank = "m" + d + c, "pb%d" % (2 + h)
+            for r in range(8):
+                at = 2048 * h + 256 * r
+                if is_abs(c, d, h, row(r, 0)):
+                    if r % 2 == 0:
+                        db = "pb%d" % ((4, 6, 5)[flip[0] % 3] if (c, h) == ("c", 1) else (4, 6)[flip[0] % 2])
+                        flip[0] += 1
+                        for i in range(2):
+                            mm(S(db, 256 * i, 256 * i + 256), S("idb", 0, 128), W(c, 128 * h, 128 * h + 128, r + i), True, False)
+                            for e in range(2):
+                                mm(S(db, 256 * i + e, 256 * i + 256, 2), S("nid"), side[d](h), False, e == 1)
+                        act(S(m, at, at + 512), S(db), AF.Abs)
+                elif (c, h) in FINE:
+                    for q in range(2):
+                        w0 = 128 * h + 64 * q
+                        tt(S(m, at + 128 * q, at + 128 * q + 128), W(c, w0, w0 + 64, r), H(dup[d], 2 * h + q), ALU.max)
+                else:
+                    tt(S(m, at, at + 256), W(c, 128 * h, 128 * h + 128, r), H(dup[d], h, 256), ALU.max)
+                f = 1 if is_abs(c, d, h, row(r, 0)) else 2
+                for e in range(2):
+                    acc(bank, row(r, e), S(m, at + e, at + 256, 2), [f * x for x in co[c, d]])
+
+        def wsum(c, h):
+            for k in range(16):
+                v = [-sum(co[c, d][i] for d in "zp" if not is_abs(c, d, h, k)) for i in range(len(co[c, "z"]))]
+                acc("pb%d" % (2 + h), k, W(c, 128 * h, 128 * h + 128, k=k), v)
+
+        def own(cs, h):
+            for d in "zp":
+                if cs == "c":
+                    n = 8 - 2 * ABS.get(("c", d, h), 0)
+                    if n:
+                        mm(H("pb%d" % (2 + h), "zp".index(d)), side[d](h), part(n))
+                    continue
+                for k in range(16):
+                    v = [-sum(co[c, d][i] for c in cs if not is_abs(c, d, h, k)) for i in range(len(co[cs[0], d]))]
+                    acc("pb%d" % (2 + h), k, side[d](h), v)
+
+        def pairs(w):
+            for j in range(16):
+                lo = 256 * (16 * w + j)
+                c = 16 * (j // 8) + 8 * w + j % 8
+                ts(S("eq", lo + 16 * j, lo + 256), S("kr", 256 * w + 16 * j, 256 * w + 256), S("gf", c, c + 1), ALU.is_equal)
+
+        for h in range(2):
+            ts(H("xg16", h, 8), H(xl, h, 8), 0.25, ALU.mult, -0.375, ALU.add)
+        ts(S("ri"), S(xl), float(t), ALU.add)
+        ts(S("ri2"), S("ri"), 15, ALU.bitwise_and)
+        cp(S("rho16"), S("ri2"))
+        act(S("mask"), gat(S("d256", 0, 16), S("rho16")), AF.Copy)
+        act(S("notm"), S("mask"), AF.Identity, 1.0, -1.0)
+        mm(S("pb4", 0, 256), S("idb", 0, 128), S("mask"), True, True)
+        mm(S("pb4", 256, 512), S("idb", 0, 128), S("notm"), True, True)
+        cp(H("a16", 0), gat(tab, H("xg16", 0, 8)))
+        for h in range(2):
+            cp(S("gf", 16 * h, 16 * h + 8), H("xg16", h, 8))
+        act(S("af"), gat(tab, S("xg16")), AF.Copy)
+        cp(H("a16", 1), H("af", 1))
+        twice("pb0", lambda a, b, z0=z0: S("prf", z0 + a, z0 + b), "zt")
+        if t == 0:
+            tt(S("x0"), gat(S(xl), S("o16")), S("d256"), ALU.mult)
+            mm(S("pb5", 256, 512), S("bof"), S("x0"), True, True)
+            xsrc, xind = "x0", "indf"
+        else:
+            xsrc, xind = "xr%d" % t, "ind16"
+            mm(S("pb5", 256, 512), S("idf"), S(xsrc), True, True)
+        ts(S("sr", 0, 256), S("idb"), S("thf", 0, 1) if t == 0 else S("scol"), ALU.mult, -1.0, ALU.mult)
+        tt(S("ma"), S("af"), S("pb4", 0, 256), ALU.mult)
+        mm(S("pb7", 0, 256), S("idb", 0, 128), S("dpen"), True, False)
+        mm(S("pb7", 0, 256), S("bof"), S("ma"), False, True)
+        mm(S("pb5", 0, 256), S("bof"), S("ma"), True, True)
+        mm(S("pb6", 0, 256), S("idf"), S("af"), True, True)
+        scan(S("ys"), S("rsmax"), S("pb7", 0, 256), 0.0, ALU.add, ALU.max)
+        ts(S("yg16"), S("ys", 15, 256, 16), 0.25, ALU.mult, -0.375, ALU.add)
+        cp(S("y16"), S("ys", 15, 256, 16))
+        act(S("bf"), gat(tab, S("yg16")), AF.Copy)
+        act(S("pp"), gat(prof, S("y16")), AF.Copy)
+        cp(S("b16"), S("bf"))
+        twice("pb1", lambda a, b: S("pp", a, b), "pt")
+        tt(S("anm"), S("af"), S("pb4", 256, 512), ALU.mult)
+        tt(S("eab"), S("bf"), S("pb6", 0, 256), ALU.is_equal)
+        ts(S("kr", 256, 512), S("pb5", 0, 256), 0.25, ALU.mult, -0.375, ALU.add)
+        ts(S("kr", 0, 256), S("pb5", 256, 512), 0.25, ALU.mult, -0.375, ALU.add)
+        for h in range(2):
+            cp(S("gf", 16 * h + 8, 16 * h + 16), H("yg16", h, 8))
+            mm(H("pb7", h, 16, 256), S("oneb"), S("chi"), True, False)
+            mm(S("pb7", 256 + 16 * h, 264 + 16 * h), H("ma", h), S("indf"))
+            mm(S("pb7", 264 + 16 * h, 272 + 16 * h), H(xsrc, h), S(xind), False, True)
+
+        def keys(h):
+            bank = "pb%d" % (2 + h)
+            mm(S(bank, 0, 384), S("oneb"), S("sr"), True, False)
+            wsum("a", h)
+            dist("a", "z", h)
+            dist("a", "p", h)
+            own("ab", h)
+            mm(S(bank, 0, 128), H("mask", h), S("bign"))
+            mm(S(bank, 0, 128), H("eab", h), S("bign"))
+            wsum("b", h)
+            dist("b", "z", h)
+            dist("b", "p", h)
+            mm(S(bank, 256, 384), H("bf", h), S("idf"), False, True)
+
+        def pick(h):
+            bank = "pb%d" % (2 + h)
+            act(H("vio", h, 256), S(bank, 0, 256), AF.Relu, 0.0, -1.0)
+            act(H("ex", h), S(bank, 256, 384), AF.Copy)
+            mm(S(bank, 256, 384), S("bign"), H("vio", 2 * h), True, False)
+            mm(S(bank, 256, 384), S("bign"), H("vio", 2 * h + 1))
+            mm(S(bank, 256, 384), S("idf"), H("ex", h), False, True)
+            act(H("sg", h), S(bank, 256, 384), AF.Sign, float(2 ** 24 + 2 ** 20))
+            scan(H("ks", h), S("rsmax", 0, 128), S(bank, 256, 384), 0.0, ALU.add, ALU.max)
+            scan(H("cs", h), S("rsmul"), H("sg", h), 0.0, ALU.mult, ALU.add)
+            nb = S("nbp", 16 * h, 16 * h + 8)
+            ts(nb, S("cs", 128 * h + 15, 128 * h + 128, 16), -12.5, ALU.is_lt, -3872.0 * 8192, ALU.mult)
+            tt(H("kk", h, 8), S("ks", 128 * h + 15, 128 * h + 128, 16), nb, ALU.add)
+            tt(H("kx", h), gat(H("kk", h, 8), S("o16", 0, 8)), S("d256", 0, 128), ALU.mult)
+            kl = S(bank, 384, 392)
+            mm(kl, H("kx", h), S("indf"), True, True)
+            ts(H("ki", h, 8), kl, -float(2 ** 25), ALU.max)
+            ts(H("brm", h, 8), kl, -16850000.0, ALU.is_gt, -8192.0, ALU.mult)
+            tt(H("fb", h, 16), H("pb7", h, 16, 256), H("nbp", h, 16), ALU.add)
+            ts(H("kg", h, 8), H("ki", h, 8), 8191, ALU.bitwise_and, 2, ALU.arith_shift_right)
+            cp(H("cg16", h, 8), H("kg", h, 8))
+            act(H("cf", h), gat(tab, H("cg16", h, 8)), AF.Copy)
+            cp(H("c16", h), H("cf", h))
+            tt(H("eqy", h), H("cf", h), H("pb5", h), ALU.is_equal)
+            tt(H("eqx", h), H("cf", h), H("pb5", 2 + h), ALU.is_equal)
+
+        def lowest(h):
+            nb = S("nbp", 16 * h, 16 * h + 8)
+            n = 128 - 64 * h
+            tt(S("rb", 128 * h, 128 * h + n), gat(H("brm", h, 8), S("o8", 0, n // 16)), S("rw", 0, n), ALU.mult)
+            tt(H("zc", h, 8), H("brm", h, 8), S("lc", 16 * t + 8 * h, 16 * t + 8 * h + 8), ALU.add)
+            for w in range(2):
+                o = S("pb7", 304 + 16 * h + 8 * w, 312 + 16 * h + 8 * w)
+                mm(o, S("nid"), nb, True, False)
+                for j in range(8 * h + 8):
+                    at = 8 * j if h == 0 else 64 + 8 * j
+                    lo = 256 * (16 * w + j) + 128 * h
+                    mm(o, S("eq", lo, lo + 128), S("rb", at, at + 8), False, j == 8 * h + 7)
+            act(H("tot", h, 16), H("pb7", h, 16, 304), AF.Copy)
+            tt(H("lose", h, 256), gat(H("tot", h, 16), S("o16")), S("thm"), ALU.is_ge)
+            for w in range(2):
+                o = S("pb7", 336 + 16 * h + 8 * w, 344 + 16 * h + 8 * w)
+                mm(o, H("lose", 2 * h + w), H("dhi", h, 8), True, False)
+                mm(o, H("lose", 2 * h + w), S("dlo"), False, True)
+            tt(H("off", h, 16), H("pb7", h, 16, 336), H("gf", h, 16), ALU.max)
+            cp(H("off16", h, 16), H("off", h, 16))
+
+        def near(h):
+            bank = "pb%d" % (2 + h)
+            mm(S(bank, 0, 256), S("oneb"), S("cr4"), True, False)
+            own("c", h)
+            wsum("c", h)
+            dist("c", "z", h)
+            dist("c", "p", h)
+            mm(S(bank, 0, 128), H("cf", h), S("idf"))
+            mm(S(bank, 128, 256), H("cf", h), S("idf"))
+            ops[-1]["late"] = ops[-2]["late"] = True
+            mm(S(bank, 0, 128), H("eqy", h), S("bigp"))
+            mm(S(bank, 128, 256), H("eqx", h), S("bigp"), False, True)
+
+        def last(h):
+            bank = rb = "pb%d" % (2 + h)
+            scan(H("ss", h, 256), S("rsmin"), S(bank, 0, 256), 0.0, ALU.add, ALU.min)
+            tt(H("vi", h, 16), S("ss", 256 * h + 15, 256 * h + 256, 16), H("fb", h, 16), ALU.min)
+            ts(H("vj", h, 16), H("vi", h, 16), 8191, ALU.bitwise_and)
+            cp(H("vf", h, 16), H("vj", h, 16))
+            tt(H("xs", h), gat(S("vj", 16 * h, 16 * h + 8), S("o16", 0, 8)), S("d256", 0, 128), ALU.mult)
+            mm(H("pb7", h, 8, 384), H("xs", h), S("indf"), True, True)
+            xn = H("sxl%d" % t, h, 8)
+            act(xn, H("pb7", h, 8, 384), AF.Copy)
+            for w in range(2):
+                act(H("ex", 2 * h + w), gat(H("vf", 2 * h + w, 8), S("o16", 0, 8)), AF.Copy)
+            mm(S(rb, 0, 128), H("ex", 2 * h), S("idf"), True, True)
+            mm(S("pb7", 0, 128), H("ex", 2 * h + 1), S("idf"), True, True)
+            tt(H("mm", h), S(rb, 0, 128), H("mask", h), ALU.mult)
+            tt(H("mm", 2 + h), S("pb7", 0, 128), H("mask", h), ALU.mult)
+            tt(gat(tab, S("off16", 16 * h, 16 * h + 8)), H("mm", h), H("anm", h), ALU.add)
+            if t < RO - 1:
+                act(H("sxr%d" % (t + 1), h), S(rb, 0, 128), AF.Copy)
+            tt(H("zo", h, 8), xn, H("zc", h, 8), ALU.max)
+            cp(H("zo16", h, 8), H("zo", h, 8))
+            act(H("zs", h), gat(S("prf", 0, z0 + NL), H("zo16", h, 8)), AF.Copy)
+            mm(S(rb, 128, 256), S("idb", 0, 128), H("zs", h), True, False)
+            mm(S(rb, 128, 256), S("idb", 0, 128), side["z"](h), False, True)
+            act(H("zh", h), S(rb, 128, 256), AF.Identity, 127.75, 0.5)
+            act(H("sz%d" % t, h), H("zh", h), AF.Identity, -128.0)
+
+        for step in STEPS:
+            stage[0] = step
+            if step[0] in "abc":
+                wgather(step[0], int(step[1]))
+            else:
+                {"k": keys, "p": pick, "e": pairs, "l": lowest, "n": near, "z": last}[step[0]](int(step[1]))
+        stage[0] = "s"
+        if t < RO - 1:
+            mm(S("pb7", 368, 384), S("cntw"), S("brm"), True, True)
+            red(S("cn"), S("pb7", 368, 384))
+            cp(S("cni"), S("cn"))
+            ts(S("cnj"), S("cni"), 15, ALU.bitwise_and)
+            ts(S("scol"), S("cnj"), S("thf", t + 1, t + 2), ALU.add)
+        for h in range(2):
+            tt(H("rg", h), gat(tab, H("yg16", h, 8)), H("notm", h), ALU.mult)
+        for h in range(2):
+            tt(gat(tab, S("off16", 16 * h + 8, 16 * h + 16)), H("rg", h), H("mm", 2 + h), ALU.add)
+        n = len(T.cores)
+        if t < RO - 1:
+            to = (rank + 1) % n
+            for h in range(2):
+                stage[0] = "z%d" % h
+                send(H("sxl%d" % t, h, 8), H("xl%d" % (t + 1), h, 8), to, "ar%d%s" % (t + 1, "lm"[h]), WIRE)
+                send(H("sz%d" % t, h), H("prf", h, 128, z0 + NL), to, "ar%d%s" % (t + 1, "zy"[h]), WIRE)
+            stage[0] = "s"
+            send(S("sxr%d" % (t + 1)), S("xr%d" % (t + 1)), to, "ar%dr" % (t + 1), WIRE)
+        else:
+            to = (rank - t) % n
+            send(S("sxl%d" % t), S("xfin"), to, "ar4l", WIRE)
+            send(S("sz%d" % t), S("zfin"), to, "ar4z", WIRE)
+    dma("s", "st0", T.ypar[:, 0:NV // 2], T.tab[:, 0:NV // 2], [S("tab", 0, NV // 2)], [], 3500)
+    dma("a", "st1", T.ypar[:, NV // 2:NV], T.tab[:, NV // 2:NV], [S("tab", NV // 2, NV)], [], 3500)
+    dma("s", "st2", T.yrec[:], S("xfin")[0], [S("xfin")], [], 2000)
+    dma("s", "st3", T.yz[:], T.zfin[:], [S("zfin")], [], 2000)
+    return pre + ops
+
+
+def depend(ops):
+    wr, rd, bank, grp = {}, {}, {}, {}
+    for i, x in enumerate(ops):
+        x["i"] = i
+        d, o = set(), set()
+        for nm, lo, hi in x["r"]:
+            d.update(j for a, b, j in wr.get(nm, ()) if a < hi and lo < b)
+        for nm, lo, hi in x["w"]:
+            d.update(j for a, b, j in wr.get(nm, ()) if a < hi and lo < b)
+            d.update(j for a, b, j in rd.get(nm, ()) if a < hi and lo < b)
+        for nm in set(r[0] for r in x["r"] + x["w"] if r[0][:2] == "pb"):
+            s = bank.setdefault(nm, [None, [], []])
+            if s[0] != x["e"]:
+                s[0], s[1], s[2] = x["e"], [], s[1]
+            s[1].append(i)
+            d.update(s[2])
+        if x["e"] == "p":
+            d = set(j for j in d if ops[j]["e"] != "p")
+            s = grp.setdefault(x["w"][0][0], [])
+            if x["start"] or x["stop"] or x.get("late"):
+                o.update(s)
+            else:
+                o.update(j for j in s if ops[j]["start"] or ops[j]["stop"] or ops[j].get("late"))
+            if x["start"]:
+                del s[:]
+            s.append(i)
+        if "after" in x:
+            o.add(x["after"]["i"])
+        for nm, lo, hi in x["w"]:
+            wr[nm] = [e for e in wr.get(nm, ()) if not (lo <= e[0] and e[1] <= hi)] + [(lo, hi, i)]
+            rd[nm] = [e for e in rd.get(nm, ()) if not (lo <= e[0] and e[1] <= hi)]
+        for nm, lo, hi in x["r"]:
+            rd.setdefault(nm, []).append((lo, hi, i))
+        d.discard(i)
+        x["d"], x["o"] = d, o
+
+
+def schedule(ops):
+    n = len(ops)
+    kids = [[] for _ in ops]
+    for x in ops:
+        for j in x["d"] | x["o"]:
+            kids[j].append(x["i"])
+
+    def gap(j, x):
+        y = ops[j]
+        if x["e"] == "x":
+            return x["lat"] if j in x["o"] else 0.0
+        if j not in x["d"]:
+            return 0.0
+        return y.get("lat", 0.0) * (y["e"] != "x") + (SELF if y["e"] == x["e"] else HOP)
+    pr = [0.0] * n
+    for x in reversed(ops):
+        i = x["i"]
+        pr[i] = x["c"] + max([gap(i, ops[k]) + pr[k] for k in kids[i]] + [x.get("lat", 0.0)])
+    fwd = [[(k, gap(i, ops[k])) for k in kids[i]] for i in range(n)]
+    back = [[(j, gap(j, x)) for j in x["d"] | x["o"]] for x in ops]
+    tail = [x.get("lat", 0.0) * (x["e"] != "x") for x in ops]
+
+    def place(seq, before, first):
+        st, en = [0.0] * n, [0.0] * n
+        busy = {e: [] for e in "vapgsx"}
+        for i in seq:
+            c, t = ops[i]["c"], first[i]
+            for j, gp in before[i]:
+                t = max(t, en[j] + gp)
+            b = busy[ops[i]["e"]]
+            lo, hi = 0, len(b)
+            while lo < hi:
+                m = (lo + hi) // 2
+                if b[m][1] <= t:
+                    lo = m + 1
+                else:
+                    hi = m
+            while c and lo < len(b) and b[lo][0] < t + c:
+                t = max(t, b[lo][1])
+                lo += 1
+            if c:
+                if lo and b[lo - 1][1] == t:
+                    b[lo - 1][1] = t + c
+                    lo -= 1
+                else:
+                    b.insert(lo, [t, t + c])
+                if lo + 1 < len(b) and b[lo + 1][0] <= t + c:
+                    b[lo][1] = b.pop(lo + 1)[1]
+            st[i], en[i] = t, t + c
+        return st, en
+    key = [BIAS.get(x["tag"], 0.0) + (50.0 * x["i"] if INLINE else -pr[x["i"]]) for x in ops]
+    if GREEDY:
+        left = [len(b) for b in back]
+        ready = {e: [] for e in "vapgsx"}
+        at, free = [0.0] * n, {e: 0.0 for e in "vapgsx"}
+        order = {e: [] for e in "vapgsx"}
+        for x in ops:
+            if not left[x["i"]]:
+                ready[x["e"]].append(x["i"])
+        soon = {e: min([at[i] for i in r] + [1e18]) for e, r in ready.items()}
+        for _ in range(n):
+            s, e = min((max(free[e], soon[e]), e) for e in ready)
+            r = ready[e]
+            i = min((key[j], j) for j in r if at[j] <= s)[1]
+            top = min((key[j], j) for j in r if at[j] <= s + AHEAD * ops[i]["c"])[1]
+            if key[top] < key[i] - ops[i]["c"]:
+                i = top
+            r.remove(i)
+            soon[e] = min([at[j] for j in r] + [1e18])
+            st = max(free[e], at[i])
+            ops[i]["t"] = (st, st + ops[i]["c"])
+            if e != "x":
+                free[e] = st + ops[i]["c"]
+            order[e].append(i)
+            for k, gp in fwd[i]:
+                at[k] = max(at[k], st + ops[i]["c"] + gp)
+                left[k] -= 1
+                if not left[k]:
+                    ready[ops[k]["e"]].append(k)
+                    soon[ops[k]["e"]] = min(soon[ops[k]["e"]], at[k])
+        return order
+    for x in ops:
+        for j in x["d"] | x["o"]:
+            key[x["i"]] = max(key[x["i"]], key[j])
+    seq, best = sorted(range(n), key=lambda i: (key[i], i)), None
+    for k in range(PASSES):
+        st, en = place(seq, back, [0.0] * n)
+        span = max(en[i] + tail[i] for i in range(n))
+        if best is None or span < best[0]:
+            best = (span, st, en)
+        if k < PASSES - 1:
+            rs, rn = place(sorted(range(n), key=lambda i: (-en[i], -i)), fwd, tail)
+            seq = sorted(range(n), key=lambda i: (-rn[i], i))
+    order = {e: [] for e in "vapgsx"}
+    for i in sorted(range(n), key=lambda i: (best[1][i], i)):
+        ops[i]["t"] = (best[1][i], best[2][i])
+        order[ops[i]["e"]].append(i)
+    return order
+
+
+def rank_program(g, core, T, topo):
+    rank = T.rank_of(core)
+    if rank is None:
+        return
+    ops = build(g, T, rank, topo)
+    depend(ops)
+    if not ORDER:
+        ORDER.update(schedule(ops))
+    order = ORDER
+    queue = {"v": g.vector, "a": g.scalar, "p": g.tensor, "g": g, "s": g.sync}
+    total = {}
+    for e in "vapg":
+        k = 0
+        for i in order[e]:
+            if "sem" not in ops[i] and "send" not in ops[i]:
+                k += 1
+                ops[i]["sem"], ops[i]["n"], ops[i]["inc"] = "q" + e, k, 1
+        total["q" + e] = k
+    for x in ops:
+        if "send" in x:
+            total["sent"] = total.get("sent", 0) + x["send"]
+        elif "inc" not in x:
+            total[x["sem"]] = x["n"]
+    seen, pos, todo = {e: {} for e in "vapgs"}, {e: 0 for e in "vapgs"}, sum(len(order[e]) for e in "vapgs")
+    for i in order["x"]:
+        ops[i]["seen"] = {}
+    while todo:
+        for e in "vapgs":
+            while pos[e] < len(order[e]) and all("seen" in ops[j] for j in ops[order[e][pos[e]]]["d"]):
+                x, need = ops[order[e][pos[e]]], {}
+                for j in x["d"]:
+                    y = ops[j]
+                    if y["n"] > need.get(y["sem"], (0, 0))[0]:
+                        need[y["sem"]] = (y["n"], j)
+                need = {s: v for s, v in need.items() if v[0] > seen[e].get(s, 0)}
+                need = {s: v for s, v in need.items() if not any(ops[w[1]]["seen"].get(s, 0) >= v[0] for u, w in need.items() if u != s)}
+                x["waits"] = sorted((s, v[0]) for s, v in need.items())
+                for s, v in need.items():
+                    seen[e][s] = v[0]
+                    for u, k in ops[v[1]]["seen"].items():
+                        seen[e][u] = max(seen[e].get(u, 0), k)
+                x["seen"] = dict(seen[e])
+                pos[e] += 1
+                todo -= 1
+    for e in "vapgs":
+        for i in order[e]:
+            x = ops[i]
+            for s, k in x["waits"]:
+                queue[e].wait_ge(T.sem[s], k)
+            ins = x["f"]()
+            if "send" not in x:
+                ins.then_inc(T.sem[x["sem"]], x.get("inc", 16))
+    for s in sorted(total):
+        g.wait_ge(T.sem[s], total[s])

@@ -7,22 +7,25 @@ F, B, I, U = "float32", "bfloat16", "int32", "uint16"
 SB = {
     "tab": (F, 2048), "pari": (I, NV), "prf": (B, NR + NL * RO), "reci": (I, 16), "thi": (I, 4), "thf": (F, 4),
     "zfin": (B, NL), "xfin": (F, 16),
-    "ia": (I, 16), "ib": (I, 16), "ct": (I, 16), "o16": (U, 16), "o8": (U, 8), "pcol": (F, 1), "rrow": (F, 256),
-    "onef": (F, 128), "idf": (F, 128), "idb": (B, 256), "nid": (B, 128), "bigp": (B, 128), "bign": (B, 128), "oneb": (B, 128),
-    "indf": (F, 8), "ind16": (F, 8), "bof": (F, 128), "bo17": (B, 128), "cntw": (F, 128), "d256": (B, 256), "dpen": (B, 256),
+    "ia": (I, 16), "ib": (I, 32), "ct": (I, 16), "o32": (U, 32), "o8": (U, 8), "pcol": (F, 1), "rrow": (F, 256),
+    "onef": (F, 128), "idf": (F, 128), "ids": (F, 128), "idb": (B, 128), "nid": (B, 128), "oneb": (B, 128),
+    "qf": (F, 128), "qs": (B, 384), "qn": (B, 128), "qbp": (B, 128), "qbn": (B, 128), "pm": (B, 1024), "hr": (B, 128), "krow": (F, 256),
+    "cr3": (B, 128), "c121": (B, 256), "bon": (B, 64), "dc": (B, 512), "zd": (B, 512), "pd": (B, 512),
+    "indf": (F, 8), "inds": (F, 8), "ind16": (F, 8), "bof": (F, 128), "bos": (F, 128), "cntw": (F, 128),
+    "d256": (B, 256), "d8k": (B, 16), "dpen": (B, 256),
     "rsmax": (B, 256), "rsmin": (B, 256), "rsmul": (B, 128), "sr": (B, 384), "cr4": (B, 256), "chi": (B, 16),
-    "rh": (B, 512), "pw": (F, 128), "tmpa": (F, 128), "tmpb": (F, 128), "c1": (F, 1), "c2": (F, 1), "rw": (F, 128), "thm": (F, 256),
-    "r8": (F, 128), "bov": (B, 384), "zt": (B, 256), "pt": (B, 256), "dhi": (B, 16), "dlo": (B, 8), "lc": (F, 64),
+    "rh": (B, 512), "pw": (F, 128), "tmpa": (F, 128), "tmpb": (F, 128), "c1": (F, 1), "c2": (F, 1), "rw": (F, 128), "thm": (F, 512),
+    "dhi": (B, 16), "dlo": (B, 8), "lc": (F, 64),
     "xg16": (U, 16), "ri": (I, 16), "ri2": (I, 16), "rho16": (U, 16), "gf": (F, 32), "kr": (U, 512), "x0": (F, 256),
-    "mask": (B, 256), "notm": (B, 256), "af": (F, 256), "bf": (F, 256), "cf": (F, 256), "a16": (U, 256), "b16": (U, 256), "c16": (U, 256),
+    "mask": (B, 256), "af": (F, 256), "bf": (F, 256), "cf": (F, 256), "a16": (U, 256), "b16": (U, 256), "c16": (U, 256),
     "ma": (F, 256), "anm": (F, 256), "ys": (F, 256), "y16": (U, 16), "yg16": (U, 16), "pp": (B, 256), "eab": (B, 256),
     "wa": (B, 4096), "wb": (B, 4096), "wc": (B, 4096),
     "mza": (B, 4096), "mpa": (B, 4096), "mzb": (B, 4096), "mpb": (B, 4096), "mzc": (B, 4096), "mpc": (B, 4096),
-    "eq": (B, 8192), "vio": (B, 512), "sg": (B, 256), "ks": (F, 256), "cs": (B, 256), "nbp": (B, 32), "kk": (F, 16), "kx": (F, 256),
+    "eq": (B, 4096), "vio": (B, 512), "sg": (B, 256), "ks": (F, 256), "cs": (B, 256), "nbp": (B, 32), "kk": (F, 16), "kx": (F, 256),
     "brm": (F, 16), "ki": (I, 16), "kg": (I, 16), "cg16": (U, 16), "fb": (F, 32), "eqy": (B, 256), "eqx": (B, 256),
-    "rb": (B, 192), "tot": (F, 32), "lose": (B, 512), "off": (F, 32), "off16": (U, 32), "zc": (F, 16),
+    "rb": (B, 128), "tot": (F, 32), "lose": (B, 512), "off": (F, 32), "off16": (U, 32), "zc": (F, 16),
     "ss": (F, 512), "vi": (I, 32), "vj": (I, 32), "vf": (F, 32), "ex": (F, 512), "mm": (F, 512), "rg": (F, 256), "xs": (F, 256),
-    "zo": (F, 16), "zo16": (U, 16), "zs": (B, 256), "zh": (B, 256), "cn": (F, 1), "cni": (I, 1), "cnj": (I, 1), "scol": (F, 1),
+    "zo": (F, 16), "zo16": (U, 16), "zs": (B, 256), "zh": (B, 256), "cj": (F, 16), "cn": (F, 1), "cni": (I, 1), "cnj": (I, 1), "scol": (F, 1),
 }
 for _t in range(RO):
     SB["xl%d" % _t] = (F, 16)
@@ -33,36 +36,46 @@ for _t in range(RO):
         SB["sxr%d" % _t] = (F, NL)
 SCRATCH, AT, _fill = {}, {}, {}
 for _k, (_d, _n) in SB.items():
-    if _n > 32:
+    if _k in ("wa", "wb", "wc", "zd", "pd"):
+        SCRATCH[_k], AT[_k] = ("sbuf", [128, _n // 2, 2], _d), (_k, 0)
+    elif _n > 32:
         SCRATCH[_k], AT[_k] = ("sbuf", [128, _n], _d), (_k, 0)
     else:
         AT[_k] = ("few" + _d, _fill.get(_d, 0))
         _fill[_d] = _fill.get(_d, 0) + (_n + 15) // 16 * 16
 for _d, _n in _fill.items():
     SCRATCH["few" + _d] = ("sbuf", [128, _n], _d)
-PSB = False
 for _b in range(8):
-    SCRATCH["pb%d" % _b] = ("psum", [128, 1024], B) if PSB and _b < 2 else ("psum", [128, 512], F)
+    SCRATCH["pb%d" % _b] = ("psum", [128, 512], F) if _b else ("psum", [128, 1024], B)
 SEMAPHORES = (["qv", "qa", "qp", "qg", "sent", "st0", "st1", "st2", "st3"] + ["ld%d" % i for i in range(6)]
-              + ["ar%d%s" % (t, w) for t in range(1, RO) for w in "lmrzy"] + ["ar4l", "ar4z"])
+              + ["ar%d%s%d" % (t, w, h) for t in range(1, RO) for w in "lrz" for h in range(2)] + ["ar4l", "ar4z"])
 
-ABS = {('a', 'p', 0): 3, ('a', 'z', 0): 1, ('b', 'p', 0): 1, ('b', 'z', 1): 2, ('c', 'p', 0): 2, ('c', 'p', 1): 3}
-WV = {('a', 1)}
-FINE = {('a', 0), ('a', 1)}
-GC, SC, CY, PC, HOP, SELF, WIRE = 1.56, 3.8, 1.0, 0.5, 120.0, 60.0, 2500.0
-TT2 = 0.5 if PSB else 1.0
-STEPS = "a0 b0 a1 b1 k0 p0 k1 c0 p1 c1 e0 e1 l0 l1 n0 n1 z0 z1".split()
-CUT = 64
-BIAS = {'svkr': 7700, 'svys': -3300, 'sapp': -2000, 'sabf': -3000, 'svcn': -5300, 'c0awc': 7700, 'svsr': -600, 'z1gsxl': -2700, 'z1gsz': -3000, 'z1ppb': -3000, 'z1vmm': -3000, 'z1vss': -3000, 'z1vtab': 5000, 'z1vvf': -4000, 'z1vvi': -2000, 'z1vvj': -3000, 'z1vxs': -6000, 'z1vzo': -3000, 'z1xprf': -3000, 'z1xxl': -3000, 'b0awb': -8000, 'svma': -1300, 'z0asxl': 3000, 'sanotm': 1000, 'p0vcs': -1000, 'saaf': -1000, 'c1awc': 3000, 'n1vmzc': -1000,
-        'sveab': -300, 'z0vss': -8000, 'svtab': -1000, 'p1avio': 300, 'p0ppb': 3000, 'p1vks': 1000, 'svcnj': -1000, 'z1asxr': 300, 'svxg': -1000, 'e0veq': -1000, 'n0vmzc': 3000, 'p1vfb': 3000, 'p1vcs': 1000, 'k0vmpa': 3000, 'k0vmpb': 3000, 'k0vmzb': 3000}
-PASSES, INLINE, GREEDY, AHEAD = 1, False, True, 0.35
+HALVES = (1, 0)
+ABS = {}
+WV = {("a", 1, 1), ("b", 1, 1)}
+CUTS = {}
+MCUT = {}
+DG = {("z", 1), ("z", 0), ("p", 0)}
+ACP = True
+GC, SC, CY, PC, FIX, HOP, SELF, WIRE = 1.56, 3.8, 0.9, 0.55, 11.0, 150.0, 70.0, 3000.0
+STEPS = "h a1 y b1 k1 a0 b0 e k0 p1 c1 p0 c0 l n1 n0 z1 z0 w".split()
+PLAN = ("w1 ub0 sa0 gc10 +bf ga00 pb0 pa0 +sc0 gb00 +ga11 +uc1 +pp +e1 +xr +gc00 +sa1 +uc0 ac +ey1 +anm +q1 r1 +y r0 +ub1 +k1 +gb10 d0 +ey0 za0 "
+        "v0 +k0 af gc01 +pa1 rho +x0 +x1 +w0 v1 +ww ua1 +e0 zb1 ex0 gb11 +pc0 eab ga10 j0 gb01 +h0 +sc1 zb0 sb0 +pb1 ex1 +ga01 gc11 +sb1 zc0 "
+        "+sr j1 +za1 +zc1 +q0 +n0 n1 lo l cn d1 +pc1 h1 +ua0 +fb").split()
+AHEAD, TT2 = 0.35, 0.5
 ORDER = {}
-K16, BIG = 65536.0, float(2 ** 26)
+K16, BIG, K13 = 65536.0, float(2 ** 26), 8192.0
+
+
+def comb(lo, hi, step):
+    if step == 1:
+        return (1 << hi) - (1 << lo)
+    return sum(1 << i for i in range(lo, hi, step))
 
 
 def build(g, T, rank, topo):
     ops, pre, rhs_at = [], [], {}
-    cur, made, stage = [ops], set(), ["s"]
+    cur, made, stage = [ops], set(), ["s", 0]
     V, A, P = g.vector, g.scalar, g.tensor
 
     def S(name, lo=0, hi=None, step=1, p=None):
@@ -72,26 +85,40 @@ def build(g, T, rank, topo):
         n = len(range(lo, hi, step))
         buf, at = AT.get(name, (name, 0))
         ap = T[buf][rows, at + lo:at + hi] if step == 1 else T[buf][rows, at + lo:at + hi:step]
-        return (ap, (name, lo, lo + (n - 1) * step + 1), n)
+        return (ap, (name, comb(lo, hi, step)), n)
 
     def two(x):
-        if x[1][0][:2] == "pb":
-            return PSB and x[1][0] in ("pb0", "pb1")
-        return SB[x[1][0]][0] in (B, U)
+        return x[1][0] == "pb0" if x[1][0][:2] == "pb" else SB[x[1][0]][0] in (B, U)
 
-    def row(r, e):
-        return 8 * e + r
+    def cells(name, lo, hi, step, e):
+        n = len(range(lo, hi, step))
+        if e is None:
+            return (T[name][:, lo:hi:step, :], (name, 3 * comb(2 * lo, 2 * hi, 2 * step)), 2 * n)
+        return (T[name][:, lo:hi:step, e], (name, comb(2 * lo + e, 2 * hi, 2 * step)), n)
 
-    def W(c, l0, l1, r=None, k=None):
-        a, st = (0, 1) if r is None and k is None else (r, 8) if k is None else (k, 16)
-        return S("w" + c, 16 * l0 + a, 16 * l1, st)
+    def W(c, l0, l1, k=0, step=1, e=None):
+        return cells("w" + c, 8 * l0 + k, 8 * l1, step, e)
+
+    def D(d, lo, hi, step=1, e=None):
+        return cells(d + "d", lo, hi, step, e)
 
     def op(eng, cost, fn, rd, wr, **kw):
-        d = {"e": eng, "c": cost, "f": fn, "r": [x[1] for x in rd], "w": [x[1] for x in wr]}
-        d["tag"] = stage[0] + eng + (wr + rd)[0][1][0].rstrip("0123456789")
+        d = {"e": eng, "k": cost, "f": fn, "r": [x[1] for x in rd], "w": [x[1] for x in wr]}
+        d["c"] = cost[1] + cost[2] * {"c": CY, "g": GC * CY, "s": SC * CY, "p": PC}[cost[0]]
+        d["c"] += FIX * (eng in "va")
+        d["tag"] = stage[0]
+        if cur[0] is pre:
+            d["key"] = -2000 if "lat" in kw else 9000
+        elif "+" + stage[0] in PLAN:
+            d["key"] = 1000 * (stage[1] - 1) + PLAN.index("+" + stage[0])
+        else:
+            d["key"] = 1000 * stage[1] + PLAN.index(stage[0])
         d.update(kw)
         cur[0].append(d)
         return d
+
+    def plain(n):
+        return ("c", 0, max(64, n), n)
 
     def gat(win, off):
         return (win[0].indirect(off[0]), win[1], off[2] * 16, off)
@@ -107,10 +134,10 @@ def build(g, T, rank, topo):
 
     def vcost(o, xs, rate):
         if len(o) == 4:
-            return 50 + SC * o[2] * CY
+            return ("s", 50, o[2])
         if len(xs[0]) == 4:
-            return 50 + GC * o[2] * CY
-        return max(64, rate * xs[0][2]) * CY
+            return ("g", 50, o[2])
+        return plain(rate * xs[0][2])
 
     def val(s):
         return s[0] if isinstance(s, tuple) else s
@@ -119,9 +146,7 @@ def build(g, T, rank, topo):
         op("v", vcost(o, [x], 0.5 if two(o) and two(x) else 1), lambda: V.tensor_copy(o[0], x[0]), rds(x), [o])
 
     def tt(o, x, y, a):
-        r = 1 if "pb" in (x[1][0][:2], y[1][0][:2]) else 2
-        if two(o) and two(x) and two(y):
-            r *= TT2
+        r = (1 if "pb" in (x[1][0][:2], y[1][0][:2]) else 2) * (TT2 if two(o) and two(x) and two(y) else 1)
         op("v", vcost(o, [x], r), lambda: V.tensor_tensor(o[0], x[0], y[0], a), rds(x, y) + rds(o)[1:], [o])
 
     def ts(o, x, s1, a, s2=None, b=None):
@@ -132,72 +157,46 @@ def build(g, T, rank, topo):
             op("v", c, lambda: V.tensor_scalar(o[0], x[0], val(s1), val(s2), a, b), rds(x, s1, s2), [o])
 
     def scan(o, d0, d1, init, a, b):
-        c = max(64, (0.5 if two(o) and two(d0) and two(d1) else 1) * o[2]) * CY
-        op("v", c, lambda: V.tensor_tensor_scan(o[0], d0[0], d1[0], init, a, b), [d0, d1], [o])
+        op("v", plain((0.5 if two(o) and two(d0) and two(d1) else 1) * o[2]), lambda: V.tensor_tensor_scan(o[0], d0[0], d1[0], init, a, b), [d0, d1], [o])
 
     def red(o, x):
-        op("v", max(64, x[2]) * CY, lambda: V.tensor_reduce(o[0], x[0], AxisListType.X, ALU.add), [x], [o])
+        op("v", plain(x[2]), lambda: V.tensor_reduce(o[0], x[0], AxisListType.X, ALU.add), [x], [o])
 
     def ms(o, c):
-        op("v", max(64, o[2] * (0.5 if two(o) else 1)) * CY, lambda: V.memset(o[0], c), [], [o])
+        op("v", plain(o[2] * (0.5 if two(o) else 1)), lambda: V.memset(o[0], c), [], [o])
 
-    def act(o, x, f, bias=0.0, scale=1.0):
-        c = 65 + GC * o[2] * CY if len(x) == 4 else max(64, o[2]) * CY
-        op("a", c, lambda: A.activation(o[0], x[0], f, bias=bias, scale=scale), rds(x), [o])
+    def act(o, x, f, bias=0.0, scale=1.0, total=None):
+        c = ("g", 65, o[2]) if len(x) == 4 else plain(o[2])
+        if total is None:
+            op("a", c, lambda: A.activation(o[0], x[0], f, bias=bias, scale=val(scale)), rds(x, scale), [o])
+        else:
+            op("a", c, lambda: A.activation(o[0], x[0], f, accum_out=total[0]), rds(x), [o, total])
 
-    def mm(o, l, r, start=False, stop=False):
-        c = max(64, r[2]) * (1 if two(r) else 4) * PC
-        op("p", c, lambda: P.matmul(o[0], l[0], r[0], start, stop), [l, r], [o], start=start, stop=stop)
-
-    def tr(o, x):
-        op("p", 128 * PC, lambda: P.transpose(o[0], x[0], S("idb", 0, 128)[0]), [x, S("idb", 0, 128)], [o], start=True, stop=True)
-
-    def twice(bank, src, tb):
-        if not PSB:
-            for h in range(2):
-                for e in range(2):
-                    mm(S(bank, 256 * h + e, 256 * h + 256, 2), S("idb", 0, 128), src(128 * h, 128 * h + 128), True, True)
-            return
-        for h in range(2):
-            tr(S(bank, 512 + 128 * h, 640 + 128 * h), src(128 * h, 128 * h + 128))
-        act(S(tb), S(bank, 512, 768), AF.Copy)
-        for h in range(2):
-            for e in range(2):
-                tr(S(bank, 256 * h + e, 256 * h + 256, 2), S(tb, 128 * h, 128 * h + 128))
-
-    def part(n):
-        if n == 8:
-            return S("bo17")
-        o = S("bov", 64 * n - 128, 64 * n)
-        if ("part", n) not in made:
-            made.add(("part", n))
-            keep, cur[0] = cur[0], pre
-            ts(S("tmpa"), S("r8"), n - 0.5, ALU.is_lt, -float(2 ** 17), ALU.mult)
-            tt(o, S("tmpa"), S("bof"), ALU.mult)
-            cur[0] = keep
-        return o
+    def mm(o, l, r, start=False, stop=False, late=False):
+        f = 1 if two(r) else 4
+        op("p", ("p", 0, max(64, r[2]) * f, r[2] * f), lambda: P.matmul(o[0], l[0], r[0], start, stop), [l, r], [o], start=start, stop=stop, late=late)
 
     def iota(o, pat, base, cm):
         if SB[o[1][0]][0] == I:
             fn = lambda: g.iota(o[0], pat, base, cm)
         else:
             fn = lambda: g.iota(o[0], pat, base, cm, allow_small_or_imprecise_dtypes=True)
-        op("g", 130 + 2 * o[2] * CY, fn, [], [o])
+        op("g", ("c", 130, 2 * o[2]), fn, [], [o])
 
     def sel(o, x, pat, cmp, base, cm):
-        op("g", 170 + 2 * o[2] * CY, lambda: g.affine_select(o[0], x[0], pat, cmp, 0.0, base, cm), [x], [o])
+        op("g", ("c", 170, 2 * o[2]), lambda: g.affine_select(o[0], x[0], pat, cmp, 0.0, base, cm), [x], [o])
 
     def dma(q, sem, dst, src, rd, wr, lat):
         e = g.sync if q == "s" else g.scalar
-        op(q, 60, lambda: e.dma_start(dst, src), rd, wr, sem=sem, n=16, lat=lat)
+        op(q, ("c", 60, 0), lambda: e.dma_start(dst, src), rd, wr, sem=sem, n=16, lat=lat)
 
-    def send(src, dst, to, sem, model):
+    def send(src, dst, to, sem):
         me, core = T.cores[rank], T.cores[to]
         rid, pid = topo.addr(core)[:2]
         eng = topo.engines(me, core)[::2]
-        d = op("g", 200, lambda: g.remote_dma(dst[0], src[0], T.sem[sem], T.sem["sent"], pid, rid, sum(1 << e for e in eng)),
+        d = op("g", ("c", 300, 0), lambda: g.remote_dma(dst[0], src[0], T.sem[sem], T.sem["sent"], pid, rid, sum(1 << e for e in eng)),
                [src], [], send=len(eng))
-        op("x", 0, None, [], [dst], sem=sem, n=len(eng), after=d, lat=model)
+        op("x", ("c", 0, 0), None, [], [dst], sem=sem, n=len(eng), after=d, lat=WIRE)
 
     def rhs(*co):
         if co not in rhs_at:
@@ -210,62 +209,73 @@ def build(g, T, rank, topo):
             cur[0] = keep
         return S("rh", rhs_at[co], rhs_at[co] + 8 * len(co))
 
-    def acc(bank, k, l, co):
-        nz = [i for i, c in enumerate(co) if c]
-        if nz:
-            a, b = nz[0], nz[-1] + 1
-            mm(S(bank, 128 * a + k, 128 * b, 16), l, rhs(*co[a:b]))
-
     cur[0] = pre
     dma("s", "ld0", S("reci")[0], T.rec[:], [], [S("reci")], 2000)
     dma("s", "ld1", T.pari[:], T.par[:], [], [S("pari")], 4500)
     dma("a", "ld2", S("thi")[0], T.th[:], [], [S("thi")], 2000)
     dma("a", "ld3", T.prf[:, NR:NR + NL], T.zf[:], [], [S("prf", NR, NR + NL)], 2200)
-    dma("s", "ld4", T.prf[:, 0:NR // 2], T.prof[:, 0:NR // 2], [], [S("prf", 0, NR // 2)], 8000)
-    dma("a", "ld5", T.prf[:, NR // 2:NR], T.prof[:, NR // 2:NR], [], [S("prf", NR // 2, NR)], 8000)
+    dma("s", "ld4", T.prf[:, 0:NR // 2], T.prof[:, 0:NR // 2], [], [S("prf", 0, NR // 2)], 9000)
+    dma("a", "ld5", T.prf[:, NR // 2:NR], T.prof[:, NR // 2:NR], [], [S("prf", NR // 2, NR)], 9000)
     ms(S("onef"), 1.0)
     iota(S("ia"), [[0, 16]], 0, 1)
-    iota(S("ib"), [[1, 16]], 0, 0)
+    iota(S("ib"), [[1, 32]], 0, 0)
     iota(S("rrow"), [[0, 16], [1, 16]], 0, 0)
-    iota(S("r8"), [[0, 16], [1, 8]], 0, 0)
+    iota(S("krow"), [[0, 16], [1, 8], [8, 2]], 0, 0)
     sel(S("idf"), S("onef"), [[-1, 128]], ALU.is_equal, 0, 1)
+    sel(S("qf"), S("onef"), [[-16, 8], [-1, 8], [-8, 2]], ALU.is_equal, 0, 1)
+    ms(S("pm", 512, 1024), 0.0)
+    for i in range(4):
+        sel(S("pm", 512 + 128 * i + 64 * (i // 2), 576 + 128 * i + 64 * (i // 2)), S("onef", 0, 64), [[-2, 64]], ALU.is_equal, -(i % 2), 1)
+    act(S("pm", 0, 512), S("pm", 512, 1024), AF.Copy, 0.0, 2 * K16)
+    act(S("pm", 512, 1024), S("pm", 512, 1024), AF.Copy, 0.0, -BIG)
+    ms(S("qs"), 0.0)
+    ms(S("sr"), 0.0)
+    for i in (0, 1, 3, 4):
+        tt(S("qs", 64 * i, 64 * i + 64), S("qf", 0, 128, 2), S("qf", 1, 128, 2), ALU.add)
+    act(S("qn"), S("qf"), AF.Copy, 0.0, -K13)
+    act(S("qbp"), S("qf"), AF.Copy, 0.0, BIG)
+    act(S("qbn"), S("qf"), AF.Copy, 0.0, -BIG)
     sel(S("tmpa"), S("onef"), [[-16, 8], [0, 16]], ALU.is_ge, 0, 1)
     sel(S("bof"), S("tmpa"), [[16, 8], [0, 16]], ALU.is_ge, 15, -1)
     for j in range(32):
         if j % 8:
-            lo = 256 * j + 128 * (j % 16 // 8)
-            iota(S("eq", lo, lo + 16 * (j % 8)), [[0, 16 * (j % 8)]], 0, 0)
+            iota(S("eq", 128 * j, 128 * j + 16 * (j % 8)), [[0, 16 * (j % 8)]], 0, 0)
     ts(S("ri"), S("ia"), 15, ALU.bitwise_and)
     cp(S("pcol"), S("ri", 0, 1))
-    cp(S("o16"), S("ib"))
-    ts(S("ct"), S("ib"), 16.0, ALU.mult, S("pcol"), ALU.add)
-    ts(S("ri2"), S("ct"), 63, ALU.bitwise_and, 3, ALU.arith_shift_right)
+    cp(S("o32"), S("ib"))
+    ts(S("ct"), S("ib", 0, 16), 16.0, ALU.mult, S("pcol"), ALU.add)
+    ts(S("ri2"), S("ct"), 3, ALU.arith_shift_right)
     cp(S("o8"), S("ri2", 0, 8))
     for t in range(RO):
         ts(S("lc", 16 * t, 16 * t + 16), S("ct"), float(NR + NL * t), ALU.add)
     ts(S("d256"), S("rrow"), S("pcol"), ALU.is_equal)
+    ts(S("d8k"), S("d256", 0, 16), K13, ALU.mult)
     ts(S("dpen"), S("d256"), -1.0, ALU.add, 16384.0, ALU.mult)
     ts(S("rsmax"), S("rrow"), 0.0, ALU.is_equal, -float(2 ** 60), ALU.mult)
     ts(S("rsmin"), S("rrow"), 0.0, ALU.is_equal, float(2 ** 60), ALU.mult)
     ts(S("rsmul"), S("rrow", 0, 128), 0.0, ALU.not_equal)
-    cp(S("idb", 0, 128), S("idf"))
-    cp(S("idb", 128, 256), S("idf"))
-    ts(S("nid"), S("idf"), -1.0, ALU.mult)
-    ts(S("bigp"), S("idf"), BIG, ALU.mult)
-    ts(S("bign"), S("idf"), -BIG, ALU.mult)
+    act(S("idb"), S("idf"), AF.Copy)
+    act(S("ids"), S("idf"), AF.Copy, 0.0, 1.0 / K13)
+    act(S("nid"), S("idf"), AF.Copy, 0.0, -1.0)
+    ts(S("c1"), S("pcol"), 7.5, ALU.is_lt)
+    ts(S("hr", 0, 128, 2), S("onef", 0, 64), S("c1"), ALU.mult)
+    ts(S("hr", 1, 128, 2), S("hr", 0, 128, 2), -1.0, ALU.mult, 1.0, ALU.add)
     ms(S("oneb"), 1.0)
-    ms(S("cntw"), -1.0 / 8192)
+    ms(S("cntw"), -1.0 / K13)
     cp(S("indf"), S("bof", 0, 128, 16))
     ts(S("ind16"), S("indf"), 1.0 / 16, ALU.mult)
-    ts(S("bo17"), S("bof"), -float(2 ** 17), ALU.mult)
-    ms(S("sr", 256, 384), 0.0)
-    ts(S("sr", 256, 384, p=0), S("rrow", 0, 128, p=0), -8192.0, ALU.mult, 15 * 8192.0, ALU.add)
-    ms(S("sr", 256, 384, p=32), -float(2 ** 24))
+    ts(S("inds"), S("indf"), 1.0 / K13, ALU.mult)
+    ts(S("bos"), S("bof"), 1.0 / K13, ALU.mult)
+    ts(S("bon"), S("bof", 0, 128, 2), -1.0, ALU.mult)
+    ms(S("cr3"), 0.0)
+    ts(S("cr3", p=0), S("krow", 0, 128, p=0), -K13, ALU.mult, 15 * K13, ALU.add)
+    ms(S("cr3", p=32), -float(2 ** 24))
     ms(S("cr4"), 0.0)
-    ts(S("cr4", p=0), S("rrow", p=0), 8192.0, ALU.mult)
-    ms(S("cr4", p=32), -121.0 * 2 ** 17)
+    ts(S("cr4", p=0), S("krow", p=0), K13, ALU.mult)
+    ms(S("c121"), 0.0)
+    ms(S("c121", p=0), -121.0)
     ms(S("chi"), 0.0)
-    ms(S("chi", p=0), 1920.0 * 8192)
+    ms(S("chi", p=0), 1920.0 * K13)
     ms(S("rh"), 0.0)
     ms(S("nbp"), 0.0)
     ms(S("tab", NV, 2048), 0.0)
@@ -276,13 +286,14 @@ def build(g, T, rank, topo):
     red(S("c1"), S("pw", 0, 16))
     for j in range(8):
         ts(S("rw", 8 * j, 8 * j + 8), S("indf"), S("c1"), ALU.mult, -(2.0 ** (-16 * j - 13)), ALU.mult)
-        ts(S("rw", 64 + 8 * j, 72 + 8 * j), S("indf"), -256.0, ALU.mult)
+    cp(S("rw", 64, 128), S("rw", 0, 64))
     tt(S("tmpb"), S("tmpa"), S("idf"), ALU.mult)
     red(S("c2"), S("tmpb"))
     ts(S("tmpa"), S("d256", 0, 128), S("c2"), ALU.mult, 2.0, ALU.mult)
     ts(S("tmpb"), S("dpen", 0, 128), -float(2 ** 26), ALU.mult)
     tt(S("thm", 0, 128), S("tmpa"), S("tmpb"), ALU.max)
-    cp(S("thm", 128, 256), S("thm", 0, 128))
+    act(S("thm", 128, 256), S("thm", 0, 128), AF.Copy)
+    act(S("thm", 256, 512), S("thm", 0, 256), AF.Copy)
     ts(S("dlo"), S("indf"), S("pcol"), ALU.mult)
     ts(S("c1"), S("ia", 0, 1), S("pcol"), ALU.subtract, float(NV), ALU.add)
     ts(S("dhi", 0, 8), S("indf"), S("c1"), ALU.mult)
@@ -290,255 +301,293 @@ def build(g, T, rank, topo):
     ts(S("dhi", 8, 16), S("indf"), S("c2"), ALU.mult)
     cp(S("xl0"), S("reci"))
     cp(S("thf"), S("thi"))
+    ts(S("scol"), S("thf", 0, 1), -1.0, ALU.mult)
     cp(S("tab", 0, NV), S("pari"))
     cur[0] = ops
 
-    tab, prof = S("tab"), S("prf", 0, NR)
-    co = {("a", "z"): (-1, 0, -K16), ("b", "z"): (1, 0, K16), ("a", "p"): (0, 1, K16), ("b", "p"): (0, -1, -K16),
-          ("c", "z"): (2 * K16, 0), ("c", "p"): (0, 2 * K16)}
+    tab, prof, o8, o16 = S("tab"), S("prf", 0, NR), S("o32", 0, 8), S("o32", 0, 16)
+    co = {("a", "z"): (-2, 0, -1), ("b", "z"): (2, 0, 1), ("a", "p"): (0, 2, 1), ("b", "p"): (0, -2, -1), ("a", "w"): (1, -1, 0), ("b", "w"): (-1, 1, 0),
+          ("c", "z"): (2, 0), ("c", "p"): (0, 2), ("c", "w"): (-1, -1)}
 
     def H(name, h, n=128, at=0):
         return S(name, at + n * h, at + n * h + n)
 
-    def is_abs(c, d, h, k):
-        return k % 8 >= 8 - 2 * ABS.get((c, d, h), 0)
+    def gene(o, x):
+        ts(o, x, 0.25, ALU.mult, -0.375, ALU.add)
 
     for t in range(RO):
         z0 = NR + NL * t
-        xl = "xl%d" % t
-        side = {"z": lambda h, z0=z0: S("prf", z0 + 128 * h, z0 + 128 * h + 128), "p": lambda h: H("pp", h)}
-        dup = {"z": "pb0", "p": "pb1"}
-        flip = [0]
+        xl, xr = "xl%d" % t, "xr%d" % t
+        side = {"z": lambda h, n=128, z0=z0: H("prf", h, n, z0), "p": lambda h, n=128: H("pp", h, n)}
+        held = {"z": lambda h: H("pb0", h, 256), "p": lambda h: H("pb0", 2 + h, 256)}
+        first, second = HALVES
+        keyb = {first: "pb1", second: "pb6"}
 
         def wgather(c, h):
-            for l in range(128 * h, 128 * h + 128, CUT):
-                src = gat(prof, S(c + "16", l, l + CUT))
-                if (c, l // 64) in WV:
-                    cp(W(c, l, l + CUT), src)
-                else:
-                    act(W(c, l, l + CUT), src, AF.Copy)
+            stage[0] = "u%s%d" % (c, h)
+            if (c, h) != ("a", first):
+                cp(H(c + "16", h), H(c + "f", h))
+            cut = CUTS.get((c, h), (0, 64))
+            for i, (a, b) in enumerate(zip(cut, cut[1:])):
+                for e in range(2):
+                    stage[0] = "g%s%d%d" % (c, h, 2 * i + e)
+                    src, dst = gat(prof, S(c + "16", 128 * h + 64 * e + a, 128 * h + 64 * e + b)), W(c, 128 * h + 2 * a, 128 * h + 2 * b, e=e)
+                    if (c, h, 2 * i + e) in WV:
+                        cp(dst, src)
+                    else:
+                        act(dst, src, AF.Copy)
 
-        def dist(c, d, h):
-            m, bank = "m" + d + c, "pb%d" % (2 + h)
+        def dist(c, d, h, stop=False):
+            m, l0, l1 = "m" + d + c, 128 * h, 128 * h + 128
+            stage[0] = "%s%s%d" % ("s" if d == "w" else d, c, h)
+            nz = [i for i, x in enumerate(co[c, d]) if x]
+            a, b, wide = nz[0], nz[-1] + 1, 64 * len(co[c, d])
             for r in range(8):
                 at = 2048 * h + 256 * r
-                if is_abs(c, d, h, row(r, 0)):
-                    if r % 2 == 0:
-                        db = "pb%d" % ((4, 6, 5)[flip[0] % 3] if (c, h) == ("c", 1) else (4, 6)[flip[0] % 2])
-                        flip[0] += 1
-                        for i in range(2):
-                            mm(S(db, 256 * i, 256 * i + 256), S("idb", 0, 128), W(c, 128 * h, 128 * h + 128, r + i), True, False)
-                            for e in range(2):
-                                mm(S(db, 256 * i + e, 256 * i + 256, 2), S("nid"), side[d](h), False, e == 1)
-                        act(S(m, at, at + 512), S(db), AF.Abs)
-                elif (c, h) in FINE:
-                    for q in range(2):
-                        w0 = 128 * h + 64 * q
-                        tt(S(m, at + 128 * q, at + 128 * q + 128), W(c, w0, w0 + 64, r), H(dup[d], 2 * h + q), ALU.max)
-                else:
-                    tt(S(m, at, at + 256), W(c, 128 * h, 128 * h + 128, r), H(dup[d], h, 256), ALU.max)
-                f = 1 if is_abs(c, d, h, row(r, 0)) else 2
+                if d != "w":
+                    tt(S(m, at, at + 256), W(c, l0, l1, r, 8), held[d](h), ALU.max)
                 for e in range(2):
-                    acc(bank, row(r, e), S(m, at + e, at + 256, 2), [f * x for x in co[c, d]])
+                    mm(S("pb%d" % (2 + h), wide * e + 64 * a + r, wide * e + 64 * b, 8), W(c, l0, l1, r, 8, e) if d == "w" else S(m, at + e, at + 256, 2),
+                       rhs(*co[c, d][a:b]), False, stop and (r, e) == (7, 1))
 
-        def wsum(c, h):
-            for k in range(16):
-                v = [-sum(co[c, d][i] for d in "zp" if not is_abs(c, d, h, k)) for i in range(len(co[c, "z"]))]
-                acc("pb%d" % (2 + h), k, W(c, 128 * h, 128 * h + 128, k=k), v)
+        def twice(d, h):
+            for i in range(4):
+                dst, src = D(d, 128 * h + i % 2, 128 * h + 128, 2, i // 2), side[d](2 * h + i // 2, 64)
+                if (d, h) in DG:
+                    sel(dst, src, [[0, 64]], ALU.is_ge, 0, 0)
+                else:
+                    act(dst, src, AF.Copy)
+            cp(held[d](h), D(d, 128 * h, 128 * h + 128))
 
-        def own(cs, h):
-            for d in "zp":
-                if cs == "c":
-                    n = 8 - 2 * ABS.get(("c", d, h), 0)
-                    if n:
-                        mm(H("pb%d" % (2 + h), "zp".index(d)), side[d](h), part(n))
-                    continue
-                for k in range(16):
-                    v = [-sum(co[c, d][i] for c in cs if not is_abs(c, d, h, k)) for i in range(len(co[cs[0], d]))]
-                    acc("pb%d" % (2 + h), k, side[d](h), v)
+        def head():
+            for h in HALVES:
+                stage[0] = "h%d" % h
+                gene(H("xg16", h, 8), H(xl, h, 8))
+                stage[0] = "d%d" % h
+                twice("z", h)
+                if h == first:
+                    stage[0] = "ua%d" % h
+                    cp(H("a16", h), gat(tab, H("xg16", h, 8)))
+                stage[0] = "ex%d" % h
+                cp(H("gf", h, 8), H("xg16", h, 8))
+            stage[0] = "rho"
+            ts(S("ri"), S(xl), float(t), ALU.add)
+            ts(S("ri2"), S("ri"), 15, ALU.bitwise_and)
+            cp(S("rho16"), S("ri2"))
+            act(S("mask"), gat(S("d8k"), S("rho16")), AF.Copy)
+            mm(S("pb4", 0, 256), S("idb"), S("mask"), True, True)
+            stage[0] = "af"
+            act(S("af"), gat(tab, S("xg16")), AF.Copy)
+            stage[0] = "xr"
+            if t == 0:
+                tt(S("x0"), gat(S(xl), o16), S("d256"), ALU.mult)
+                mm(S("pb5", 256, 512), S("bof"), S("x0"), True, True)
+                gene(S("kr", 0, 256), S("pb5", 256, 512))
+            else:
+                for h in HALVES:
+                    stage[0] = "ex%d" % h
+                    gene(H("kr", h), H(xr, h))
+            stage[0] = "sr"
+            act(S("sr", 0, 320), S("qs", 0, 320), AF.Copy, 0.0, S("scol"))
 
-        def pairs(w):
-            for j in range(16):
-                lo = 256 * (16 * w + j)
-                c = 16 * (j // 8) + 8 * w + j % 8
-                ts(S("eq", lo + 16 * j, lo + 256), S("kr", 256 * w + 16 * j, 256 * w + 256), S("gf", c, c + 1), ALU.is_equal)
+        def partner():
+            stage[0] = "y"
+            tt(S("ma"), S("af"), S("pb4", 0, 256), ALU.mult)
+            mm(S("pb7", 0, 256), S("idb"), S("dpen"), True, False)
+            mm(S("pb7", 0, 256), S("bos"), S("ma"), False, True)
+            mm(S("pb5", 0, 256), S("bos"), S("ma"), True, True)
+            scan(S("ys"), S("rsmax"), S("pb7", 0, 256), 0.0, ALU.add, ALU.max)
+            gene(S("yg16"), S("ys", 15, 256, 16))
+            cp(S("y16"), S("ys", 15, 256, 16))
+            stage[0] = "bf"
+            act(S("bf"), gat(tab, S("yg16")), AF.Copy)
+            stage[0] = "pp"
+            act(S("pp"), gat(prof, S("y16")), AF.Copy)
+            for h in HALVES:
+                stage[0] = "e%d" % h
+                twice("p", h)
+            stage[0] = "ac"
+            if ACP:
+                mm(S("pb6", 0, 256), S("idf"), S("af"), True, True)
+            else:
+                act(S("pb6", 0, 256), S("af"), AF.Copy)
+            stage[0] = "anm"
+            tt(S("anm"), S("af"), S("pb4", 0, 256), ALU.subtract)
+            stage[0] = "eab"
+            tt(S("eab"), S("bf"), S("pb6", 0, 256), ALU.is_equal)
+            stage[0] = "ey1"
+            gene(S("kr", 256, 512), S("pb5", 0, 256))
+            cp(S("gf", 16, 32), S("yg16"))
+            stage[0] = "xr"
+            if t:
+                act(S("pb5", 256, 512), S(xr), AF.Copy)
+            stage[0] = "fb"
+            xsrc, xind = ("x0", "indf") if t == 0 else (xr, "ind16")
+            for h in HALVES:
+                mm(H("pb7", h, 16, 256), S("oneb"), S("chi"), True, False)
+                mm(S("pb7", 256 + 16 * h, 264 + 16 * h), H("ma", h), S("inds"))
+                mm(S("pb7", 264 + 16 * h, 272 + 16 * h), H(xsrc, h), S(xind), False, True)
 
-        for h in range(2):
-            ts(H("xg16", h, 8), H(xl, h, 8), 0.25, ALU.mult, -0.375, ALU.add)
-        ts(S("ri"), S(xl), float(t), ALU.add)
-        ts(S("ri2"), S("ri"), 15, ALU.bitwise_and)
-        cp(S("rho16"), S("ri2"))
-        act(S("mask"), gat(S("d256", 0, 16), S("rho16")), AF.Copy)
-        act(S("notm"), S("mask"), AF.Identity, 1.0, -1.0)
-        mm(S("pb4", 0, 256), S("idb", 0, 128), S("mask"), True, True)
-        mm(S("pb4", 256, 512), S("idb", 0, 128), S("notm"), True, True)
-        cp(H("a16", 0), gat(tab, H("xg16", 0, 8)))
-        for h in range(2):
-            cp(S("gf", 16 * h, 16 * h + 8), H("xg16", h, 8))
-        act(S("af"), gat(tab, S("xg16")), AF.Copy)
-        cp(H("a16", 1), H("af", 1))
-        twice("pb0", lambda a, b, z0=z0: S("prf", z0 + a, z0 + b), "zt")
-        if t == 0:
-            tt(S("x0"), gat(S(xl), S("o16")), S("d256"), ALU.mult)
-            mm(S("pb5", 256, 512), S("bof"), S("x0"), True, True)
-            xsrc, xind = "x0", "indf"
-        else:
-            xsrc, xind = "xr%d" % t, "ind16"
-            mm(S("pb5", 256, 512), S("idf"), S(xsrc), True, True)
-        ts(S("sr", 0, 256), S("idb"), S("thf", 0, 1) if t == 0 else S("scol"), ALU.mult, -1.0, ALU.mult)
-        tt(S("ma"), S("af"), S("pb4", 0, 256), ALU.mult)
-        mm(S("pb7", 0, 256), S("idb", 0, 128), S("dpen"), True, False)
-        mm(S("pb7", 0, 256), S("bof"), S("ma"), False, True)
-        mm(S("pb5", 0, 256), S("bof"), S("ma"), True, True)
-        mm(S("pb6", 0, 256), S("idf"), S("af"), True, True)
-        scan(S("ys"), S("rsmax"), S("pb7", 0, 256), 0.0, ALU.add, ALU.max)
-        ts(S("yg16"), S("ys", 15, 256, 16), 0.25, ALU.mult, -0.375, ALU.add)
-        cp(S("y16"), S("ys", 15, 256, 16))
-        act(S("bf"), gat(tab, S("yg16")), AF.Copy)
-        act(S("pp"), gat(prof, S("y16")), AF.Copy)
-        cp(S("b16"), S("bf"))
-        twice("pb1", lambda a, b: S("pp", a, b), "pt")
-        tt(S("anm"), S("af"), S("pb4", 256, 512), ALU.mult)
-        tt(S("eab"), S("bf"), S("pb6", 0, 256), ALU.is_equal)
-        ts(S("kr", 256, 512), S("pb5", 0, 256), 0.25, ALU.mult, -0.375, ALU.add)
-        ts(S("kr", 0, 256), S("pb5", 256, 512), 0.25, ALU.mult, -0.375, ALU.add)
-        for h in range(2):
-            cp(S("gf", 16 * h + 8, 16 * h + 16), H("yg16", h, 8))
-            mm(H("pb7", h, 16, 256), S("oneb"), S("chi"), True, False)
-            mm(S("pb7", 256 + 16 * h, 264 + 16 * h), H("ma", h), S("indf"))
-            mm(S("pb7", 264 + 16 * h, 272 + 16 * h), H(xsrc, h), S(xind), False, True)
+        def pairs():
+            for w in range(2):
+                for h in HALVES:
+                    stage[0] = "e%s%d" % ("xy"[w], h)
+                    for j in range(8):
+                        lo, c = 128 * (16 * w + 8 * h + j), 16 * w + 8 * h + j
+                        ts(S("eq", lo + 16 * j, lo + 128), S("kr", 16 * c, 256 * w + 128 * h + 128), S("gf", c, c + 1), ALU.is_equal)
 
         def keys(h):
-            bank = "pb%d" % (2 + h)
-            mm(S(bank, 0, 384), S("oneb"), S("sr"), True, False)
-            wsum("a", h)
-            dist("a", "z", h)
-            dist("a", "p", h)
-            own("ab", h)
-            mm(S(bank, 0, 128), H("mask", h), S("bign"))
-            mm(S(bank, 0, 128), H("eab", h), S("bign"))
-            wsum("b", h)
-            dist("b", "z", h)
-            dist("b", "p", h)
-            mm(S(bank, 256, 384), H("bf", h), S("idf"), False, True)
+            stage[0] = "za%d" % h
+            mm(S("pb%d" % (2 + h), 0, 384), S("hr"), S("sr"), True, False)
+            for c in "ab":
+                dist(c, "w", h)
+                dist(c, "z", h)
+                dist(c, "p", h, c == "b")
+            stage[0] = "j%d" % h
+            key = S(keyb[h], 0, 128)
+            mm(key, S("oneb"), S("cr3"), True, False)
+            mm(key, H("bf", h), S("qf"))
+            mm(key, H("mask", h), S("qn"))
+            mm(key, H("eab", h), S("qbn"))
 
         def pick(h):
-            bank = "pb%d" % (2 + h)
-            act(H("vio", h, 256), S(bank, 0, 256), AF.Relu, 0.0, -1.0)
-            act(H("ex", h), S(bank, 256, 384), AF.Copy)
-            mm(S(bank, 256, 384), S("bign"), H("vio", 2 * h), True, False)
-            mm(S(bank, 256, 384), S("bign"), H("vio", 2 * h + 1))
-            mm(S(bank, 256, 384), S("idf"), H("ex", h), False, True)
-            act(H("sg", h), S(bank, 256, 384), AF.Sign, float(2 ** 24 + 2 ** 20))
-            scan(H("ks", h), S("rsmax", 0, 128), S(bank, 256, 384), 0.0, ALU.add, ALU.max)
+            bank, key = "pb%d" % (2 + h), S(keyb[h], 0, 128)
+            stage[0] = "k%d" % h
+            for e in range(2):
+                act(H("vio", 2 * h + e), S(bank, 192 * e, 192 * e + 128), AF.Relu, 0.0, -1.0)
+                act(H("dc", 4 * h + e, 64), S(bank, 192 * e + 128, 192 * e + 192), AF.Copy)
+            for i in range(4):
+                o = S(keyb[h], i % 2, 128, 2)
+                mm(o, H("pm", i), H("dc", 4 * h + i // 2, 64))
+                for w in range(2):
+                    mm(o, H("pm", 4 + i), H("vio", 4 * h + 2 * (i // 2) + w, 64), False, (i, w) == (3, 1))
+            act(H("sg", h), key, AF.Sign, float(2 ** 24 + 2 ** 20))
+            scan(H("ks", h), S("rsmax", 0, 128), key, 0.0, ALU.add, ALU.max)
             scan(H("cs", h), S("rsmul"), H("sg", h), 0.0, ALU.mult, ALU.add)
             nb = S("nbp", 16 * h, 16 * h + 8)
-            ts(nb, S("cs", 128 * h + 15, 128 * h + 128, 16), -12.5, ALU.is_lt, -3872.0 * 8192, ALU.mult)
+            ts(nb, S("cs", 128 * h + 15, 128 * h + 128, 16), -12.5, ALU.is_lt, -3872.0 * K13, ALU.mult)
             tt(H("kk", h, 8), S("ks", 128 * h + 15, 128 * h + 128, 16), nb, ALU.add)
-            tt(H("kx", h), gat(H("kk", h, 8), S("o16", 0, 8)), S("d256", 0, 128), ALU.mult)
-            kl = S(bank, 384, 392)
+            tt(H("kx", h), gat(H("kk", h, 8), o8), S("d256", 0, 128), ALU.mult)
+            kl = H("pb7", h, 8, 288)
             mm(kl, H("kx", h), S("indf"), True, True)
             ts(H("ki", h, 8), kl, -float(2 ** 25), ALU.max)
-            ts(H("brm", h, 8), kl, -16850000.0, ALU.is_gt, -8192.0, ALU.mult)
-            tt(H("fb", h, 16), H("pb7", h, 16, 256), H("nbp", h, 16), ALU.add)
             ts(H("kg", h, 8), H("ki", h, 8), 8191, ALU.bitwise_and, 2, ALU.arith_shift_right)
             cp(H("cg16", h, 8), H("kg", h, 8))
             act(H("cf", h), gat(tab, H("cg16", h, 8)), AF.Copy)
-            cp(H("c16", h), H("cf", h))
+            stage[0] = "q%d" % h
             tt(H("eqy", h), H("cf", h), H("pb5", h), ALU.is_equal)
             tt(H("eqx", h), H("cf", h), H("pb5", 2 + h), ALU.is_equal)
 
-        def lowest(h):
-            nb = S("nbp", 16 * h, 16 * h + 8)
-            n = 128 - 64 * h
-            tt(S("rb", 128 * h, 128 * h + n), gat(H("brm", h, 8), S("o8", 0, n // 16)), S("rw", 0, n), ALU.mult)
-            tt(H("zc", h, 8), H("brm", h, 8), S("lc", 16 * t + 8 * h, 16 * t + 8 * h + 8), ALU.add)
-            for w in range(2):
-                o = S("pb7", 304 + 16 * h + 8 * w, 312 + 16 * h + 8 * w)
-                mm(o, S("nid"), nb, True, False)
-                for j in range(8 * h + 8):
-                    at = 8 * j if h == 0 else 64 + 8 * j
-                    lo = 256 * (16 * w + j) + 128 * h
-                    mm(o, S("eq", lo, lo + 128), S("rb", at, at + 8), False, j == 8 * h + 7)
-            act(H("tot", h, 16), H("pb7", h, 16, 304), AF.Copy)
-            tt(H("lose", h, 256), gat(H("tot", h, 16), S("o16")), S("thm"), ALU.is_ge)
-            for w in range(2):
-                o = S("pb7", 336 + 16 * h + 8 * w, 344 + 16 * h + 8 * w)
-                mm(o, H("lose", 2 * h + w), H("dhi", h, 8), True, False)
-                mm(o, H("lose", 2 * h + w), S("dlo"), False, True)
-            tt(H("off", h, 16), H("pb7", h, 16, 336), H("gf", h, 16), ALU.max)
-            cp(H("off16", h, 16), H("off", h, 16))
+        def lowest():
+            stage[0] = "l"
+            ts(S("brm"), S("pb7", 288, 304), -16850000.0, ALU.is_gt, -K13, ALU.mult)
+            tt(S("fb"), S("pb7", 256, 288), S("nbp"), ALU.add)
+            tt(S("rb"), gat(S("brm"), S("o8")), S("rw"), ALU.mult)
+            tt(S("zc"), S("brm"), S("lc", 16 * t, 16 * t + 16), ALU.add)
+            for h in HALVES:
+                for w in range(2):
+                    o = H("pb7", 2 * h + w, 8, 304)
+                    mm(o, S("nid"), S("nbp", 16 * h, 16 * h + 8), True, False)
+                    for j in range(8):
+                        mm(o, H("eq", 16 * w + 8 * h + j), H("rb", 8 * h + j, 8), False, j == 7)
+            if t < RO - 1:
+                mm(S("pb7", 368, 384), S("cntw"), S("brm"), True, True)
+            act(S("tot"), S("pb7", 304, 336), AF.Copy)
+            if t < RO - 1:
+                act(S("cj"), S("pb7", 368, 384), AF.Identity, total=S("cn"))
+            stage[0] = "lo"
+            tt(S("lose"), gat(S("tot"), S("o32")), S("thm"), ALU.is_ge)
+            for h in HALVES:
+                for w in range(2):
+                    o = H("pb7", 2 * w + h, 8, 336)
+                    mm(o, H("lose", 2 * h + w), H("dhi", h, 8), True, False)
+                    mm(o, H("lose", 2 * h + w), S("dlo"), False, True)
+            tt(S("off"), S("pb7", 336, 368), S("gf"), ALU.max)
+            cp(S("off16"), S("off"))
+            if t < RO - 1:
+                stage[0] = "cn"
+                cp(S("cni"), S("cn"))
+                ts(S("cnj"), S("cni"), 15, ALU.bitwise_and)
+                ts(S("scol"), S("cnj"), S("thf", t + 1, t + 2), ALU.add, -1.0, ALU.mult)
 
         def near(h):
-            bank = "pb%d" % (2 + h)
-            mm(S(bank, 0, 256), S("oneb"), S("cr4"), True, False)
-            own("c", h)
-            wsum("c", h)
-            dist("c", "z", h)
-            dist("c", "p", h)
-            mm(S(bank, 0, 128), H("cf", h), S("idf"))
-            mm(S(bank, 128, 256), H("cf", h), S("idf"))
-            ops[-1]["late"] = ops[-2]["late"] = True
-            mm(S(bank, 0, 128), H("eqy", h), S("bigp"))
-            mm(S(bank, 128, 256), H("eqx", h), S("bigp"), False, True)
+            bank, kb = "pb%d" % (2 + h), keyb[h]
+            stage[0] = "zc%d" % h
+            mm(S(bank, 0, 256), S("oneb"), S("c121"), True, False)
+            for i, d in enumerate("zp"):
+                for e in range(2):
+                    mm(H(bank, 2 * e + i, 64), D(d, 128 * h, 128 * h + 128, 1, e), S("bon"))
+            for d in "wzp":
+                dist("c", d, h, d == "p")
+            stage[0] = "q%d" % h
+            mm(S(kb, 0, 256), S("oneb"), S("cr4"), True, False)
+            for i, d in enumerate("yx"):
+                mm(H(kb, i), H("cf", h), S("qf"))
+                mm(H(kb, i), H("eq" + d, h), S("qbp"))
+            stage[0] = "n%d" % h
+            act(H("dc", h, 256), S(bank, 0, 256), AF.Copy)
+            for i in range(4):
+                mm(S(kb, i % 2, 256, 2), H("pm", i), H("dc", 2 * h + i // 2), False, i == 3)
 
         def last(h):
-            bank = rb = "pb%d" % (2 + h)
-            scan(H("ss", h, 256), S("rsmin"), S(bank, 0, 256), 0.0, ALU.add, ALU.min)
+            bank = "pb%d" % (2 + h)
+            stage[0] = "n%d" % h
+            scan(H("ss", h, 256), S("rsmin"), S(keyb[h], 0, 256), 0.0, ALU.add, ALU.min)
             tt(H("vi", h, 16), S("ss", 256 * h + 15, 256 * h + 256, 16), H("fb", h, 16), ALU.min)
             ts(H("vj", h, 16), H("vi", h, 16), 8191, ALU.bitwise_and)
             cp(H("vf", h, 16), H("vj", h, 16))
-            tt(H("xs", h), gat(S("vj", 16 * h, 16 * h + 8), S("o16", 0, 8)), S("d256", 0, 128), ALU.mult)
+            stage[0] = "x%d" % h
+            tt(H("xs", h), gat(S("vj", 16 * h, 16 * h + 8), o8), S("d256", 0, 128), ALU.mult)
             mm(H("pb7", h, 8, 384), H("xs", h), S("indf"), True, True)
             xn = H("sxl%d" % t, h, 8)
             act(xn, H("pb7", h, 8, 384), AF.Copy)
-            for w in range(2):
-                act(H("ex", 2 * h + w), gat(H("vf", 2 * h + w, 8), S("o16", 0, 8)), AF.Copy)
-            mm(S(rb, 0, 128), H("ex", 2 * h), S("idf"), True, True)
-            mm(S("pb7", 0, 128), H("ex", 2 * h + 1), S("idf"), True, True)
-            tt(H("mm", h), S(rb, 0, 128), H("mask", h), ALU.mult)
-            tt(H("mm", 2 + h), S("pb7", 0, 128), H("mask", h), ALU.mult)
-            tt(gat(tab, S("off16", 16 * h, 16 * h + 8)), H("mm", h), H("anm", h), ALU.add)
+            to = (rank + 1) % len(T.cores)
             if t < RO - 1:
-                act(H("sxr%d" % (t + 1), h), S(rb, 0, 128), AF.Copy)
+                send(xn, H("xl%d" % (t + 1), h, 8), to, "ar%dl%d" % (t + 1, h))
+            stage[0] = "w%d" % h
+            if h == first:
+                act(H("ex", h, 256), gat(H("vf", h, 16), o16), AF.Copy)
+            else:
+                for w in range(2):
+                    act(H("ex", 2 * h + w), gat(H("vf", 2 * h + w, 8), o8), AF.Copy)
+            for w in range(2):
+                mm(H(bank, w), H("ex", 2 * h + w), S("ids"), True, True)
+            for w in range(2):
+                tt(H("mm", 2 * w + h), H(bank, w), H("mask", h), ALU.mult)
+            tt(gat(tab, H("off16", h, 8)), H("mm", h), H("anm", h), ALU.max)
+            stage[0] = "r%d" % h
+            if t < RO - 1:
+                act(H("sxr%d" % (t + 1), h), H(bank, 0), AF.Copy, 0.0, K13)
+                send(H("sxr%d" % (t + 1), h), H("xr%d" % (t + 1), h), to, "ar%dr%d" % (t + 1, h))
+            stage[0] = "v%d" % h
             tt(H("zo", h, 8), xn, H("zc", h, 8), ALU.max)
             cp(H("zo16", h, 8), H("zo", h, 8))
             act(H("zs", h), gat(S("prf", 0, z0 + NL), H("zo16", h, 8)), AF.Copy)
-            mm(S(rb, 128, 256), S("idb", 0, 128), H("zs", h), True, False)
-            mm(S(rb, 128, 256), S("idb", 0, 128), side["z"](h), False, True)
-            act(H("zh", h), S(rb, 128, 256), AF.Identity, 127.75, 0.5)
+            mm(H(bank, 2), S("idb"), H("zs", h), True, False)
+            mm(H(bank, 2), S("idb"), side["z"](h), False, True)
+            act(H("zh", h), H(bank, 2), AF.Identity, 127.75, 0.5)
             act(H("sz%d" % t, h), H("zh", h), AF.Identity, -128.0)
+            if t < RO - 1:
+                send(H("sz%d" % t, h), H("prf", h, 128, z0 + NL), to, "ar%dz%d" % (t + 1, h))
 
+        def writes():
+            stage[0] = "ww"
+            tt(S("rg"), gat(tab, S("yg16")), S("mask"), ALU.subtract)
+            for h in HALVES:
+                tt(gat(tab, H("off16", 2 + h, 8)), H("rg", h), H("mm", 2 + h), ALU.max)
+
+        stage[1] = t
         for step in STEPS:
-            stage[0] = step
             if step[0] in "abc":
                 wgather(step[0], int(step[1]))
+            elif len(step) == 1:
+                {"h": head, "y": partner, "e": pairs, "l": lowest, "w": writes}[step]()
             else:
-                {"k": keys, "p": pick, "e": pairs, "l": lowest, "n": near, "z": last}[step[0]](int(step[1]))
-        stage[0] = "s"
-        if t < RO - 1:
-            mm(S("pb7", 368, 384), S("cntw"), S("brm"), True, True)
-            red(S("cn"), S("pb7", 368, 384))
-            cp(S("cni"), S("cn"))
-            ts(S("cnj"), S("cni"), 15, ALU.bitwise_and)
-            ts(S("scol"), S("cnj"), S("thf", t + 1, t + 2), ALU.add)
-        for h in range(2):
-            tt(H("rg", h), gat(tab, H("yg16", h, 8)), H("notm", h), ALU.mult)
-        for h in range(2):
-            tt(gat(tab, S("off16", 16 * h + 8, 16 * h + 16)), H("rg", h), H("mm", 2 + h), ALU.add)
-        n = len(T.cores)
-        if t < RO - 1:
-            to = (rank + 1) % n
-            for h in range(2):
-                stage[0] = "z%d" % h
-                send(H("sxl%d" % t, h, 8), H("xl%d" % (t + 1), h, 8), to, "ar%d%s" % (t + 1, "lm"[h]), WIRE)
-                send(H("sz%d" % t, h), H("prf", h, 128, z0 + NL), to, "ar%d%s" % (t + 1, "zy"[h]), WIRE)
-            stage[0] = "s"
-            send(S("sxr%d" % (t + 1)), S("xr%d" % (t + 1)), to, "ar%dr" % (t + 1), WIRE)
-        else:
-            to = (rank - t) % n
-            send(S("sxl%d" % t), S("xfin"), to, "ar4l", WIRE)
-            send(S("sz%d" % t), S("zfin"), to, "ar4z", WIRE)
+                {"k": keys, "p": pick, "n": near, "z": last}[step[0]](int(step[1]))
+    stage[0] = "ww"
+    home = (rank - RO + 1) % len(T.cores)
+    send(S("sxl%d" % (RO - 1)), S("xfin"), home, "ar4l")
+    send(S("sz%d" % (RO - 1)), S("zfin"), home, "ar4z")
     dma("s", "st0", T.ypar[:, 0:NV // 2], T.tab[:, 0:NV // 2], [S("tab", 0, NV // 2)], [], 3500)
     dma("a", "st1", T.ypar[:, NV // 2:NV], T.tab[:, NV // 2:NV], [S("tab", NV // 2, NV)], [], 3500)
     dma("s", "st2", T.yrec[:], S("xfin")[0], [S("xfin")], [], 2000)
@@ -551,11 +600,11 @@ def depend(ops):
     for i, x in enumerate(ops):
         x["i"] = i
         d, o = set(), set()
-        for nm, lo, hi in x["r"]:
-            d.update(j for a, b, j in wr.get(nm, ()) if a < hi and lo < b)
-        for nm, lo, hi in x["w"]:
-            d.update(j for a, b, j in wr.get(nm, ()) if a < hi and lo < b)
-            d.update(j for a, b, j in rd.get(nm, ()) if a < hi and lo < b)
+        for nm, m in x["r"]:
+            d.update(j for a, j in wr.get(nm, ()) if a & m)
+        for nm, m in x["w"]:
+            d.update(j for a, j in wr.get(nm, ()) if a & m)
+            d.update(j for a, j in rd.get(nm, ()) if a & m)
         for nm in set(r[0] for r in x["r"] + x["w"] if r[0][:2] == "pb"):
             s = bank.setdefault(nm, [None, [], []])
             if s[0] != x["e"]:
@@ -565,30 +614,26 @@ def depend(ops):
         if x["e"] == "p":
             d = set(j for j in d if ops[j]["e"] != "p")
             s = grp.setdefault(x["w"][0][0], [])
-            if x["start"] or x["stop"] or x.get("late"):
+            if x["start"] or x["stop"] or x["late"]:
                 o.update(s)
             else:
-                o.update(j for j in s if ops[j]["start"] or ops[j]["stop"] or ops[j].get("late"))
+                o.update(j for j in s if ops[j]["start"] or ops[j]["stop"] or ops[j]["late"])
             if x["start"]:
                 del s[:]
             s.append(i)
         if "after" in x:
             o.add(x["after"]["i"])
-        for nm, lo, hi in x["w"]:
-            wr[nm] = [e for e in wr.get(nm, ()) if not (lo <= e[0] and e[1] <= hi)] + [(lo, hi, i)]
-            rd[nm] = [e for e in rd.get(nm, ()) if not (lo <= e[0] and e[1] <= hi)]
-        for nm, lo, hi in x["r"]:
-            rd.setdefault(nm, []).append((lo, hi, i))
+        for nm, m in x["w"]:
+            wr[nm] = [(a & ~m, j) for a, j in wr.get(nm, ()) if a & ~m] + [(m, i)]
+            rd[nm] = [(a & ~m, j) for a, j in rd.get(nm, ()) if a & ~m]
+        for nm, m in x["r"]:
+            rd.setdefault(nm, []).append((m, i))
         d.discard(i)
         x["d"], x["o"] = d, o
 
 
 def schedule(ops):
     n = len(ops)
-    kids = [[] for _ in ops]
-    for x in ops:
-        for j in x["d"] | x["o"]:
-            kids[j].append(x["i"])
 
     def gap(j, x):
         y = ops[j]
@@ -597,90 +642,44 @@ def schedule(ops):
         if j not in x["d"]:
             return 0.0
         return y.get("lat", 0.0) * (y["e"] != "x") + (SELF if y["e"] == x["e"] else HOP)
-    pr = [0.0] * n
-    for x in reversed(ops):
-        i = x["i"]
-        pr[i] = x["c"] + max([gap(i, ops[k]) + pr[k] for k in kids[i]] + [x.get("lat", 0.0)])
-    fwd = [[(k, gap(i, ops[k])) for k in kids[i]] for i in range(n)]
     back = [[(j, gap(j, x)) for j in x["d"] | x["o"]] for x in ops]
+    fwd = [[] for _ in ops]
+    for i in range(n):
+        for j, gp in back[i]:
+            fwd[j].append((i, gp))
     tail = [x.get("lat", 0.0) * (x["e"] != "x") for x in ops]
 
-    def place(seq, before, first):
-        st, en = [0.0] * n, [0.0] * n
-        busy = {e: [] for e in "vapgsx"}
-        for i in seq:
-            c, t = ops[i]["c"], first[i]
-            for j, gp in before[i]:
-                t = max(t, en[j] + gp)
-            b = busy[ops[i]["e"]]
-            lo, hi = 0, len(b)
-            while lo < hi:
-                m = (lo + hi) // 2
-                if b[m][1] <= t:
-                    lo = m + 1
-                else:
-                    hi = m
-            while c and lo < len(b) and b[lo][0] < t + c:
-                t = max(t, b[lo][1])
-                lo += 1
-            if c:
-                if lo and b[lo - 1][1] == t:
-                    b[lo - 1][1] = t + c
-                    lo -= 1
-                else:
-                    b.insert(lo, [t, t + c])
-                if lo + 1 < len(b) and b[lo + 1][0] <= t + c:
-                    b[lo][1] = b.pop(lo + 1)[1]
-            st[i], en[i] = t, t + c
-        return st, en
-    key = [BIAS.get(x["tag"], 0.0) + (50.0 * x["i"] if INLINE else -pr[x["i"]]) for x in ops]
-    if GREEDY:
-        left = [len(b) for b in back]
-        ready = {e: [] for e in "vapgsx"}
-        at, free = [0.0] * n, {e: 0.0 for e in "vapgsx"}
-        order = {e: [] for e in "vapgsx"}
-        for x in ops:
-            if not left[x["i"]]:
-                ready[x["e"]].append(x["i"])
+    def run(key, before, after, first):
+        left, at, end = [len(b) for b in before], list(first), [0.0] * n
+        ready, free, order = {e: [] for e in "vapgsx"}, {e: 0.0 for e in "vapgsx"}, {e: [] for e in "vapgsx"}
+        for i in range(n):
+            if not left[i]:
+                ready[ops[i]["e"]].append(i)
         soon = {e: min([at[i] for i in r] + [1e18]) for e, r in ready.items()}
         for _ in range(n):
             s, e = min((max(free[e], soon[e]), e) for e in ready)
             r = ready[e]
             i = min((key[j], j) for j in r if at[j] <= s)[1]
             top = min((key[j], j) for j in r if at[j] <= s + AHEAD * ops[i]["c"])[1]
-            if key[top] < key[i] - ops[i]["c"]:
+            if key[top] < key[i]:
                 i = top
             r.remove(i)
             soon[e] = min([at[j] for j in r] + [1e18])
-            st = max(free[e], at[i])
-            ops[i]["t"] = (st, st + ops[i]["c"])
+            end[i] = max(free[e], at[i]) + ops[i]["c"]
             if e != "x":
-                free[e] = st + ops[i]["c"]
+                free[e] = end[i]
             order[e].append(i)
-            for k, gp in fwd[i]:
-                at[k] = max(at[k], st + ops[i]["c"] + gp)
+            for k, gp in after[i]:
+                at[k] = max(at[k], end[i] + gp)
                 left[k] -= 1
                 if not left[k]:
                     ready[ops[k]["e"]].append(k)
                     soon[ops[k]["e"]] = min(soon[ops[k]["e"]], at[k])
-        return order
-    for x in ops:
-        for j in x["d"] | x["o"]:
-            key[x["i"]] = max(key[x["i"]], key[j])
-    seq, best = sorted(range(n), key=lambda i: (key[i], i)), None
-    for k in range(PASSES):
-        st, en = place(seq, back, [0.0] * n)
-        span = max(en[i] + tail[i] for i in range(n))
-        if best is None or span < best[0]:
-            best = (span, st, en)
-        if k < PASSES - 1:
-            rs, rn = place(sorted(range(n), key=lambda i: (-en[i], -i)), fwd, tail)
-            seq = sorted(range(n), key=lambda i: (-rn[i], i))
-    order = {e: [] for e in "vapgsx"}
-    for i in sorted(range(n), key=lambda i: (best[1][i], i)):
-        ops[i]["t"] = (best[1][i], best[2][i])
-        order[ops[i]["e"]].append(i)
-    return order
+        return end, order
+    key = [x["key"] for x in ops]
+    for i in range(n - 1, -1, -1):
+        key[i] = min([key[i]] + [key[k] for k, gp in fwd[i]])
+    return run(key, back, fwd, [0.0] * n)[1]
 
 
 def rank_program(g, core, T, topo):

from concourse.mybir import AluOpType, AxisListType, ActivationFunctionType

ALU, AF = AluOpType, ActivationFunctionType

NV, NR, NL, RO = 1536, 6144, 256, 4
F, B, I, U = "float32", "bfloat16", "int32", "uint16"
SB = {
    "tab": (F, 2048), "pari": (I, NV), "prf": (B, NR + NL * RO), "reci": (I, 16), "thi": (I, 4), "thf": (F, 4),
    "zfin": (B, NL), "xfin": (F, 16),
    "ia": (I, 16), "ib": (I, 32), "ct": (I, 16), "o32": (U, 32), "o8": (U, 8), "pcol": (F, 1), "rrow": (F, 256),
    "onef": (F, 128), "idf": (F, 128), "ids": (F, 128), "idb": (B, 128), "nid": (B, 128), "oneb": (B, 128),
    "qf": (F, 128), "qs": (B, 384), "qn": (B, 128), "qbp": (B, 128), "qbn": (B, 128), "pm": (B, 1024), "hr": (B, 128), "krow": (F, 256),
    "cr3": (B, 128), "c121": (B, 256), "bon": (B, 64), "dc": (B, 512), "zd": (B, 512), "pd": (B, 512),
    "indf": (F, 8), "inds": (F, 8), "ind16": (F, 8), "bof": (F, 128), "bos": (F, 128), "cntw": (F, 128),
    "d256": (B, 256), "d8k": (B, 16), "dpen": (B, 256),
    "rsmax": (B, 256), "rsmin": (B, 256), "rsmul": (B, 128), "sr": (B, 384), "cr4": (B, 256), "chi": (B, 16),
    "rh": (B, 512), "pw": (F, 128), "tmpa": (F, 128), "tmpb": (F, 128), "c1": (F, 1), "c2": (F, 1), "rw": (F, 128), "thm": (F, 512),
    "dhi": (B, 16), "dlo": (B, 8), "lc": (F, 64),
    "xg16": (U, 16), "ri": (I, 16), "ri2": (I, 16), "rho16": (U, 16), "gf": (F, 32), "kr": (U, 512), "x0": (F, 256),
    "mask": (B, 256), "af": (F, 256), "bf": (F, 256), "cf": (F, 256), "a16": (U, 256), "b16": (U, 256), "c16": (U, 256),
    "ma": (F, 256), "anm": (F, 256), "ys": (F, 256), "y16": (U, 16), "yg16": (U, 16), "pp": (B, 256), "eab": (B, 256),
    "wa": (B, 4096), "wb": (B, 4096), "wc": (B, 4096),
    "mza": (B, 4096), "mpa": (B, 4096), "mzb": (B, 4096), "mpb": (B, 4096), "mzc": (B, 4096), "mpc": (B, 4096),
    "eq": (B, 4096), "vio": (B, 512), "sg": (B, 256), "ks": (F, 256), "cs": (B, 256), "nbp": (B, 32), "kk": (F, 16), "kx": (F, 256),
    "brm": (F, 16), "ki": (I, 16), "kg": (I, 16), "cg16": (U, 16), "fb": (F, 32), "eqy": (B, 256), "eqx": (B, 256),
    "rb": (B, 128), "tot": (F, 32), "lose": (B, 512), "off": (F, 32), "off16": (U, 32), "zc": (F, 16),
    "ss": (F, 512), "vi": (I, 32), "vj": (I, 32), "vf": (F, 32), "ex": (F, 512), "mm": (F, 512), "rg": (F, 256), "xs": (F, 256),
    "zo": (F, 16), "zo16": (U, 16), "zs": (B, 256), "zh": (B, 256), "cj": (F, 16), "cn": (F, 1), "cni": (I, 1), "cnj": (I, 1), "scol": (F, 1),
}
for _t in range(RO):
    SB["xl%d" % _t] = (F, 16)
    SB["sxl%d" % _t] = (F, 16)
    SB["sz%d" % _t] = (B, NL)
    if _t:
        SB["xr%d" % _t] = (F, NL)
        SB["sxr%d" % _t] = (F, NL)
SCRATCH, AT, _fill = {}, {}, {}
for _k, (_d, _n) in SB.items():
    if _k in ("wa", "wb", "wc", "zd", "pd"):
        SCRATCH[_k], AT[_k] = ("sbuf", [128, _n // 2, 2], _d), (_k, 0)
    elif _n > 32:
        SCRATCH[_k], AT[_k] = ("sbuf", [128, _n], _d), (_k, 0)
    else:
        AT[_k] = ("few" + _d, _fill.get(_d, 0))
        _fill[_d] = _fill.get(_d, 0) + (_n + 15) // 16 * 16
for _d, _n in _fill.items():
    SCRATCH["few" + _d] = ("sbuf", [128, _n], _d)
for _b in range(8):
    SCRATCH["pb%d" % _b] = ("psum", [128, 512], F) if _b else ("psum", [128, 1024], B)
SEMAPHORES = (["qv", "qa", "qp", "qg", "sent", "st0", "st1", "st2", "st3"] + ["ld%d" % i for i in range(6)]
              + ["ar%d%s%d" % (t, w, h) for t in range(1, RO) for w in "lrz" for h in range(2)] + ["ar4l", "ar4z"])

HALVES = (1, 0)
ABS = {}
WV = {("a", 1, 1), ("b", 1, 1)}
CUTS = {}
MCUT = {}
DG = {("z", 1), ("z", 0), ("p", 0)}
ACP = True
GC, SC, CY, PC, FIX, HOP, SELF, WIRE = 1.56, 3.8, 0.9, 0.55, 11.0, 150.0, 70.0, 3000.0
STEPS = "h a1 y b1 k1 a0 b0 e k0 p1 c1 p0 c0 l n1 n0 z1 z0 w".split()
PLAN = ("w1 ub0 sa0 gc10 +bf ga00 pb0 pa0 +sc0 gb00 +ga11 +uc1 +pp +e1 +xr +gc00 +sa1 +uc0 ac +ey1 +anm +q1 r1 +y r0 +ub1 +k1 +gb10 d0 +ey0 za0 "
        "v0 +k0 af gc01 +pa1 rho +x0 +x1 +w0 v1 +ww ua1 +e0 zb1 ex0 gb11 +pc0 eab ga10 j0 gb01 +h0 +sc1 zb0 sb0 +pb1 ex1 +ga01 gc11 +sb1 zc0 "
        "+sr j1 +za1 +zc1 +q0 +n0 n1 lo l cn d1 +pc1 h1 +ua0 +fb").split()
AHEAD, TT2 = 0.35, 0.5
ORDER = {}
K16, BIG, K13 = 65536.0, float(2 ** 26), 8192.0


def comb(lo, hi, step):
    if step == 1:
        return (1 << hi) - (1 << lo)
    return sum(1 << i for i in range(lo, hi, step))


def build(g, T, rank, topo):
    ops, pre, rhs_at = [], [], {}
    cur, made, stage = [ops], set(), ["s", 0]
    V, A, P = g.vector, g.scalar, g.tensor

    def S(name, lo=0, hi=None, step=1, p=None):
        if hi is None:
            hi = 512 if name[:2] == "pb" else SB[name][1]
        rows = slice(None) if p is None else slice(p, p + 1)
        n = len(range(lo, hi, step))
        buf, at = AT.get(name, (name, 0))
        ap = T[buf][rows, at + lo:at + hi] if step == 1 else T[buf][rows, at + lo:at + hi:step]
        return (ap, (name, comb(lo, hi, step)), n)

    def two(x):
        return x[1][0] == "pb0" if x[1][0][:2] == "pb" else SB[x[1][0]][0] in (B, U)

    def cells(name, lo, hi, step, e):
        n = len(range(lo, hi, step))
        if e is None:
            return (T[name][:, lo:hi:step, :], (name, 3 * comb(2 * lo, 2 * hi, 2 * step)), 2 * n)
        return (T[name][:, lo:hi:step, e], (name, comb(2 * lo + e, 2 * hi, 2 * step)), n)

    def W(c, l0, l1, k=0, step=1, e=None):
        return cells("w" + c, 8 * l0 + k, 8 * l1, step, e)

    def D(d, lo, hi, step=1, e=None):
        return cells(d + "d", lo, hi, step, e)

    def op(eng, cost, fn, rd, wr, **kw):
        d = {"e": eng, "k": cost, "f": fn, "r": [x[1] for x in rd], "w": [x[1] for x in wr]}
        d["c"] = cost[1] + cost[2] * {"c": CY, "g": GC * CY, "s": SC * CY, "p": PC}[cost[0]]
        d["c"] += FIX * (eng in "va")
        d["tag"] = stage[0]
        if cur[0] is pre:
            d["key"] = -2000 if "lat" in kw else 9000
        elif "+" + stage[0] in PLAN:
            d["key"] = 1000 * (stage[1] - 1) + PLAN.index("+" + stage[0])
        else:
            d["key"] = 1000 * stage[1] + PLAN.index(stage[0])
        d.update(kw)
        cur[0].append(d)
        return d

    def plain(n):
        return ("c", 0, max(64, n), n)

    def gat(win, off):
        return (win[0].indirect(off[0]), win[1], off[2] * 16, off)

    def rds(*xs):
        out = []
        for x in xs:
            if isinstance(x, tuple):
                out.append(x)
                if len(x) == 4:
                    out.append(x[3])
        return out

    def vcost(o, xs, rate):
        if len(o) == 4:
            return ("s", 50, o[2])
        if len(xs[0]) == 4:
            return ("g", 50, o[2])
        return plain(rate * xs[0][2])

    def val(s):
        return s[0] if isinstance(s, tuple) else s

    def cp(o, x):
        op("v", vcost(o, [x], 0.5 if two(o) and two(x) else 1), lambda: V.tensor_copy(o[0], x[0]), rds(x), [o])

    def tt(o, x, y, a):
        r = (1 if "pb" in (x[1][0][:2], y[1][0][:2]) else 2) * (TT2 if two(o) and two(x) and two(y) else 1)
        op("v", vcost(o, [x], r), lambda: V.tensor_tensor(o[0], x[0], y[0], a), rds(x, y) + rds(o)[1:], [o])

    def ts(o, x, s1, a, s2=None, b=None):
        c = vcost(o, [x], 0.5 if two(o) and two(x) else 1)
        if b is None:
            op("v", c, lambda: V.tensor_scalar(o[0], x[0], val(s1), None, a), rds(x, s1), [o])
        else:
            op("v", c, lambda: V.tensor_scalar(o[0], x[0], val(s1), val(s2), a, b), rds(x, s1, s2), [o])

    def scan(o, d0, d1, init, a, b):
        op("v", plain((0.5 if two(o) and two(d0) and two(d1) else 1) * o[2]), lambda: V.tensor_tensor_scan(o[0], d0[0], d1[0], init, a, b), [d0, d1], [o])

    def red(o, x):
        op("v", plain(x[2]), lambda: V.tensor_reduce(o[0], x[0], AxisListType.X, ALU.add), [x], [o])

    def ms(o, c):
        op("v", plain(o[2] * (0.5 if two(o) else 1)), lambda: V.memset(o[0], c), [], [o])

    def act(o, x, f, bias=0.0, scale=1.0, total=None):
        c = ("g", 65, o[2]) if len(x) == 4 else plain(o[2])
        if total is None:
            op("a", c, lambda: A.activation(o[0], x[0], f, bias=bias, scale=val(scale)), rds(x, scale), [o])
        else:
            op("a", c, lambda: A.activation(o[0], x[0], f, accum_out=total[0]), rds(x), [o, total])

    def mm(o, l, r, start=False, stop=False, late=False):
        f = 1 if two(r) else 4
        op("p", ("p", 0, max(64, r[2]) * f, r[2] * f), lambda: P.matmul(o[0], l[0], r[0], start, stop), [l, r], [o], start=start, stop=stop, late=late)

    def iota(o, pat, base, cm):
        if SB[o[1][0]][0] == I:
            fn = lambda: g.iota(o[0], pat, base, cm)
        else:
            fn = lambda: g.iota(o[0], pat, base, cm, allow_small_or_imprecise_dtypes=True)
        op("g", ("c", 130, 2 * o[2]), fn, [], [o])

    def sel(o, x, pat, cmp, base, cm):
        op("g", ("c", 170, 2 * o[2]), lambda: g.affine_select(o[0], x[0], pat, cmp, 0.0, base, cm), [x], [o])

    def dma(q, sem, dst, src, rd, wr, lat):
        e = g.sync if q == "s" else g.scalar
        op(q, ("c", 60, 0), lambda: e.dma_start(dst, src), rd, wr, sem=sem, n=16, lat=lat)

    def send(src, dst, to, sem):
        me, core = T.cores[rank], T.cores[to]
        rid, pid = topo.addr(core)[:2]
        eng = topo.engines(me, core)[::2]
        d = op("g", ("c", 300, 0), lambda: g.remote_dma(dst[0], src[0], T.sem[sem], T.sem["sent"], pid, rid, sum(1 << e for e in eng)),
               [src], [], send=len(eng))
        op("x", ("c", 0, 0), None, [], [dst], sem=sem, n=len(eng), after=d, lat=WIRE)

    def rhs(*co):
        if co not in rhs_at:
            at = sum(len(c) for c in rhs_at) * 8
            rhs_at[co] = at
            keep, cur[0] = cur[0], pre
            for i, c in enumerate(co):
                if c:
                    ts(S("rh", at + 8 * i, at + 8 * i + 8), S("indf"), float(c), ALU.mult)
            cur[0] = keep
        return S("rh", rhs_at[co], rhs_at[co] + 8 * len(co))

    cur[0] = pre
    dma("s", "ld0", S("reci")[0], T.rec[:], [], [S("reci")], 2000)
    dma("s", "ld1", T.pari[:], T.par[:], [], [S("pari")], 4500)
    dma("a", "ld2", S("thi")[0], T.th[:], [], [S("thi")], 2000)
    dma("a", "ld3", T.prf[:, NR:NR + NL], T.zf[:], [], [S("prf", NR, NR + NL)], 2200)
    dma("s", "ld4", T.prf[:, 0:NR // 2], T.prof[:, 0:NR // 2], [], [S("prf", 0, NR // 2)], 9000)
    dma("a", "ld5", T.prf[:, NR // 2:NR], T.prof[:, NR // 2:NR], [], [S("prf", NR // 2, NR)], 9000)
    ms(S("onef"), 1.0)
    iota(S("ia"), [[0, 16]], 0, 1)
    iota(S("ib"), [[1, 32]], 0, 0)
    iota(S("rrow"), [[0, 16], [1, 16]], 0, 0)
    iota(S("krow"), [[0, 16], [1, 8], [8, 2]], 0, 0)
    sel(S("idf"), S("onef"), [[-1, 128]], ALU.is_equal, 0, 1)
    sel(S("qf"), S("onef"), [[-16, 8], [-1, 8], [-8, 2]], ALU.is_equal, 0, 1)
    ms(S("pm", 512, 1024), 0.0)
    for i in range(4):
        sel(S("pm", 512 + 128 * i + 64 * (i // 2), 576 + 128 * i + 64 * (i // 2)), S("onef", 0, 64), [[-2, 64]], ALU.is_equal, -(i % 2), 1)
    act(S("pm", 0, 512), S("pm", 512, 1024), AF.Copy, 0.0, 2 * K16)
    act(S("pm", 512, 1024), S("pm", 512, 1024), AF.Copy, 0.0, -BIG)
    ms(S("qs"), 0.0)
    ms(S("sr"), 0.0)
    for i in (0, 1, 3, 4):
        tt(S("qs", 64 * i, 64 * i + 64), S("qf", 0, 128, 2), S("qf", 1, 128, 2), ALU.add)
    act(S("qn"), S("qf"), AF.Copy, 0.0, -K13)
    act(S("qbp"), S("qf"), AF.Copy, 0.0, BIG)
    act(S("qbn"), S("qf"), AF.Copy, 0.0, -BIG)
    sel(S("tmpa"), S("onef"), [[-16, 8], [0, 16]], ALU.is_ge, 0, 1)
    sel(S("bof"), S("tmpa"), [[16, 8], [0, 16]], ALU.is_ge, 15, -1)
    for j in range(32):
        if j % 8:
            iota(S("eq", 128 * j, 128 * j + 16 * (j % 8)), [[0, 16 * (j % 8)]], 0, 0)
    ts(S("ri"), S("ia"), 15, ALU.bitwise_and)
    cp(S("pcol"), S("ri", 0, 1))
    cp(S("o32"), S("ib"))
    ts(S("ct"), S("ib", 0, 16), 16.0, ALU.mult, S("pcol"), ALU.add)
    ts(S("ri2"), S("ct"), 3, ALU.arith_shift_right)
    cp(S("o8"), S("ri2", 0, 8))
    for t in range(RO):
        ts(S("lc", 16 * t, 16 * t + 16), S("ct"), float(NR + NL * t), ALU.add)
    ts(S("d256"), S("rrow"), S("pcol"), ALU.is_equal)
    ts(S("d8k"), S("d256", 0, 16), K13, ALU.mult)
    ts(S("dpen"), S("d256"), -1.0, ALU.add, 16384.0, ALU.mult)
    ts(S("rsmax"), S("rrow"), 0.0, ALU.is_equal, -float(2 ** 60), ALU.mult)
    ts(S("rsmin"), S("rrow"), 0.0, ALU.is_equal, float(2 ** 60), ALU.mult)
    ts(S("rsmul"), S("rrow", 0, 128), 0.0, ALU.not_equal)
    act(S("idb"), S("idf"), AF.Copy)
    act(S("ids"), S("idf"), AF.Copy, 0.0, 1.0 / K13)
    act(S("nid"), S("idf"), AF.Copy, 0.0, -1.0)
    ts(S("c1"), S("pcol"), 7.5, ALU.is_lt)
    ts(S("hr", 0, 128, 2), S("onef", 0, 64), S("c1"), ALU.mult)
    ts(S("hr", 1, 128, 2), S("hr", 0, 128, 2), -1.0, ALU.mult, 1.0, ALU.add)
    ms(S("oneb"), 1.0)
    ms(S("cntw"), -1.0 / K13)
    cp(S("indf"), S("bof", 0, 128, 16))
    ts(S("ind16"), S("indf"), 1.0 / 16, ALU.mult)
    ts(S("inds"), S("indf"), 1.0 / K13, ALU.mult)
    ts(S("bos"), S("bof"), 1.0 / K13, ALU.mult)
    ts(S("bon"), S("bof", 0, 128, 2), -1.0, ALU.mult)
    ms(S("cr3"), 0.0)
    ts(S("cr3", p=0), S("krow", 0, 128, p=0), -K13, ALU.mult, 15 * K13, ALU.add)
    ms(S("cr3", p=32), -float(2 ** 24))
    ms(S("cr4"), 0.0)
    ts(S("cr4", p=0), S("krow", p=0), K13, ALU.mult)
    ms(S("c121"), 0.0)
    ms(S("c121", p=0), -121.0)
    ms(S("chi"), 0.0)
    ms(S("chi", p=0), 1920.0 * K13)
    ms(S("rh"), 0.0)
    ms(S("nbp"), 0.0)
    ms(S("tab", NV, 2048), 0.0)
    ts(S("pw"), S("onef"), 0.5, ALU.mult)
    ms(S("tmpb"), 0.0)
    scan(S("tmpa"), S("pw"), S("tmpb"), float(2 ** 21), ALU.mult, ALU.add)
    tt(S("pw", 0, 16), S("tmpa", 0, 16), S("d256", 0, 16), ALU.mult)
    red(S("c1"), S("pw", 0, 16))
    for j in range(8):
        ts(S("rw", 8 * j, 8 * j + 8), S("indf"), S("c1"), ALU.mult, -(2.0 ** (-16 * j - 13)), ALU.mult)
    cp(S("rw", 64, 128), S("rw", 0, 64))
    tt(S("tmpb"), S("tmpa"), S("idf"), ALU.mult)
    red(S("c2"), S("tmpb"))
    ts(S("tmpa"), S("d256", 0, 128), S("c2"), ALU.mult, 2.0, ALU.mult)
    ts(S("tmpb"), S("dpen", 0, 128), -float(2 ** 26), ALU.mult)
    tt(S("thm", 0, 128), S("tmpa"), S("tmpb"), ALU.max)
    act(S("thm", 128, 256), S("thm", 0, 128), AF.Copy)
    act(S("thm", 256, 512), S("thm", 0, 256), AF.Copy)
    ts(S("dlo"), S("indf"), S("pcol"), ALU.mult)
    ts(S("c1"), S("ia", 0, 1), S("pcol"), ALU.subtract, float(NV), ALU.add)
    ts(S("dhi", 0, 8), S("indf"), S("c1"), ALU.mult)
    ts(S("c2"), S("c1"), 128.0, ALU.add)
    ts(S("dhi", 8, 16), S("indf"), S("c2"), ALU.mult)
    cp(S("xl0"), S("reci"))
    cp(S("thf"), S("thi"))
    ts(S("scol"), S("thf", 0, 1), -1.0, ALU.mult)
    cp(S("tab", 0, NV), S("pari"))
    cur[0] = ops

    tab, prof, o8, o16 = S("tab"), S("prf", 0, NR), S("o32", 0, 8), S("o32", 0, 16)
    co = {("a", "z"): (-2, 0, -1), ("b", "z"): (2, 0, 1), ("a", "p"): (0, 2, 1), ("b", "p"): (0, -2, -1), ("a", "w"): (1, -1, 0), ("b", "w"): (-1, 1, 0),
          ("c", "z"): (2, 0), ("c", "p"): (0, 2), ("c", "w"): (-1, -1)}

    def H(name, h, n=128, at=0):
        return S(name, at + n * h, at + n * h + n)

    def gene(o, x):
        ts(o, x, 0.25, ALU.mult, -0.375, ALU.add)

    for t in range(RO):
        z0 = NR + NL * t
        xl, xr = "xl%d" % t, "xr%d" % t
        side = {"z": lambda h, n=128, z0=z0: H("prf", h, n, z0), "p": lambda h, n=128: H("pp", h, n)}
        held = {"z": lambda h: H("pb0", h, 256), "p": lambda h: H("pb0", 2 + h, 256)}
        first, second = HALVES
        keyb = {first: "pb1", second: "pb6"}

        def wgather(c, h):
            stage[0] = "u%s%d" % (c, h)
            if (c, h) != ("a", first):
                cp(H(c + "16", h), H(c + "f", h))
            cut = CUTS.get((c, h), (0, 64))
            for i, (a, b) in enumerate(zip(cut, cut[1:])):
                for e in range(2):
                    stage[0] = "g%s%d%d" % (c, h, 2 * i + e)
                    src, dst = gat(prof, S(c + "16", 128 * h + 64 * e + a, 128 * h + 64 * e + b)), W(c, 128 * h + 2 * a, 128 * h + 2 * b, e=e)
                    if (c, h, 2 * i + e) in WV:
                        cp(dst, src)
                    else:
                        act(dst, src, AF.Copy)

        def dist(c, d, h, stop=False):
            m, l0, l1 = "m" + d + c, 128 * h, 128 * h + 128
            stage[0] = "%s%s%d" % ("s" if d == "w" else d, c, h)
            nz = [i for i, x in enumerate(co[c, d]) if x]
            a, b, wide = nz[0], nz[-1] + 1, 64 * len(co[c, d])
            for r in range(8):
                at = 2048 * h + 256 * r
                if d != "w":
                    tt(S(m, at, at + 256), W(c, l0, l1, r, 8), held[d](h), ALU.max)
                for e in range(2):
                    mm(S("pb%d" % (2 + h), wide * e + 64 * a + r, wide * e + 64 * b, 8), W(c, l0, l1, r, 8, e) if d == "w" else S(m, at + e, at + 256, 2),
                       rhs(*co[c, d][a:b]), False, stop and (r, e) == (7, 1))

        def twice(d, h):
            for i in range(4):
                dst, src = D(d, 128 * h + i % 2, 128 * h + 128, 2, i // 2), side[d](2 * h + i // 2, 64)
                if (d, h) in DG:
                    sel(dst, src, [[0, 64]], ALU.is_ge, 0, 0)
                else:
                    act(dst, src, AF.Copy)
            cp(held[d](h), D(d, 128 * h, 128 * h + 128))

        def head():
            for h in HALVES:
                stage[0] = "h%d" % h
                gene(H("xg16", h, 8), H(xl, h, 8))
                stage[0] = "d%d" % h
                twice("z", h)
                if h == first:
                    stage[0] = "ua%d" % h
                    cp(H("a16", h), gat(tab, H("xg16", h, 8)))
                stage[0] = "ex%d" % h
                cp(H("gf", h, 8), H("xg16", h, 8))
            stage[0] = "rho"
            ts(S("ri"), S(xl), float(t), ALU.add)
            ts(S("ri2"), S("ri"), 15, ALU.bitwise_and)
            cp(S("rho16"), S("ri2"))
            act(S("mask"), gat(S("d8k"), S("rho16")), AF.Copy)
            mm(S("pb4", 0, 256), S("idb"), S("mask"), True, True)
            stage[0] = "af"
            act(S("af"), gat(tab, S("xg16")), AF.Copy)
            stage[0] = "xr"
            if t == 0:
                tt(S("x0"), gat(S(xl), o16), S("d256"), ALU.mult)
                mm(S("pb5", 256, 512), S("bof"), S("x0"), True, True)
                gene(S("kr", 0, 256), S("pb5", 256, 512))
            else:
                for h in HALVES:
                    stage[0] = "ex%d" % h
                    gene(H("kr", h), H(xr, h))
            stage[0] = "sr"
            act(S("sr", 0, 320), S("qs", 0, 320), AF.Copy, 0.0, S("scol"))

        def partner():
            stage[0] = "y"
            tt(S("ma"), S("af"), S("pb4", 0, 256), ALU.mult)
            mm(S("pb7", 0, 256), S("idb"), S("dpen"), True, False)
            mm(S("pb7", 0, 256), S("bos"), S("ma"), False, True)
            mm(S("pb5", 0, 256), S("bos"), S("ma"), True, True)
            scan(S("ys"), S("rsmax"), S("pb7", 0, 256), 0.0, ALU.add, ALU.max)
            gene(S("yg16"), S("ys", 15, 256, 16))
            cp(S("y16"), S("ys", 15, 256, 16))
            stage[0] = "bf"
            act(S("bf"), gat(tab, S("yg16")), AF.Copy)
            stage[0] = "pp"
            act(S("pp"), gat(prof, S("y16")), AF.Copy)
            for h in HALVES:
                stage[0] = "e%d" % h
                twice("p", h)
            stage[0] = "ac"
            if ACP:
                mm(S("pb6", 0, 256), S("idf"), S("af"), True, True)
            else:
                act(S("pb6", 0, 256), S("af"), AF.Copy)
            stage[0] = "anm"
            tt(S("anm"), S("af"), S("pb4", 0, 256), ALU.subtract)
            stage[0] = "eab"
            tt(S("eab"), S("bf"), S("pb6", 0, 256), ALU.is_equal)
            stage[0] = "ey1"
            gene(S("kr", 256, 512), S("pb5", 0, 256))
            cp(S("gf", 16, 32), S("yg16"))
            stage[0] = "xr"
            if t:
                act(S("pb5", 256, 512), S(xr), AF.Copy)
            stage[0] = "fb"
            xsrc, xind = ("x0", "indf") if t == 0 else (xr, "ind16")
            for h in HALVES:
                mm(H("pb7", h, 16, 256), S("oneb"), S("chi"), True, False)
                mm(S("pb7", 256 + 16 * h, 264 + 16 * h), H("ma", h), S("inds"))
                mm(S("pb7", 264 + 16 * h, 272 + 16 * h), H(xsrc, h), S(xind), False, True)

        def pairs():
            for w in range(2):
                for h in HALVES:
                    stage[0] = "e%s%d" % ("xy"[w], h)
                    for j in range(8):
                        lo, c = 128 * (16 * w + 8 * h + j), 16 * w + 8 * h + j
                        ts(S("eq", lo + 16 * j, lo + 128), S("kr", 16 * c, 256 * w + 128 * h + 128), S("gf", c, c + 1), ALU.is_equal)

        def keys(h):
            stage[0] = "za%d" % h
            mm(S("pb%d" % (2 + h), 0, 384), S("hr"), S("sr"), True, False)
            for c in "ab":
                dist(c, "w", h)
                dist(c, "z", h)
                dist(c, "p", h, c == "b")
            stage[0] = "j%d" % h
            key = S(keyb[h], 0, 128)
            mm(key, S("oneb"), S("cr3"), True, False)
            mm(key, H("bf", h), S("qf"))
            mm(key, H("mask", h), S("qn"))
            mm(key, H("eab", h), S("qbn"))

        def pick(h):
            bank, key = "pb%d" % (2 + h), S(keyb[h], 0, 128)
            stage[0] = "k%d" % h
            for e in range(2):
                act(H("vio", 2 * h + e), S(bank, 192 * e, 192 * e + 128), AF.Relu, 0.0, -1.0)
                act(H("dc", 4 * h + e, 64), S(bank, 192 * e + 128, 192 * e + 192), AF.Copy)
            for i in range(4):
                o = S(keyb[h], i % 2, 128, 2)
                mm(o, H("pm", i), H("dc", 4 * h + i // 2, 64))
                for w in range(2):
                    mm(o, H("pm", 4 + i), H("vio", 4 * h + 2 * (i // 2) + w, 64), False, (i, w) == (3, 1))
            act(H("sg", h), key, AF.Sign, float(2 ** 24 + 2 ** 20))
            scan(H("ks", h), S("rsmax", 0, 128), key, 0.0, ALU.add, ALU.max)
            scan(H("cs", h), S("rsmul"), H("sg", h), 0.0, ALU.mult, ALU.add)
            nb = S("nbp", 16 * h, 16 * h + 8)
            ts(nb, S("cs", 128 * h + 15, 128 * h + 128, 16), -12.5, ALU.is_lt, -3872.0 * K13, ALU.mult)
            tt(H("kk", h, 8), S("ks", 128 * h + 15, 128 * h + 128, 16), nb, ALU.add)
            tt(H("kx", h), gat(H("kk", h, 8), o8), S("d256", 0, 128), ALU.mult)
            kl = H("pb7", h, 8, 288)
            mm(kl, H("kx", h), S("indf"), True, True)
            ts(H("ki", h, 8), kl, -float(2 ** 25), ALU.max)
            ts(H("kg", h, 8), H("ki", h, 8), 8191, ALU.bitwise_and, 2, ALU.arith_shift_right)
            cp(H("cg16", h, 8), H("kg", h, 8))
            act(H("cf", h), gat(tab, H("cg16", h, 8)), AF.Copy)
            stage[0] = "q%d" % h
            tt(H("eqy", h), H("cf", h), H("pb5", h), ALU.is_equal)
            tt(H("eqx", h), H("cf", h), H("pb5", 2 + h), ALU.is_equal)

        def lowest():
            stage[0] = "l"
            ts(S("brm"), S("pb7", 288, 304), -16850000.0, ALU.is_gt, -K13, ALU.mult)
            tt(S("fb"), S("pb7", 256, 288), S("nbp"), ALU.add)
            tt(S("rb"), gat(S("brm"), S("o8")), S("rw"), ALU.mult)
            tt(S("zc"), S("brm"), S("lc", 16 * t, 16 * t + 16), ALU.add)
            for h in HALVES:
                for w in range(2):
                    o = H("pb7", 2 * h + w, 8, 304)
                    mm(o, S("nid"), S("nbp", 16 * h, 16 * h + 8), True, False)
                    for j in range(8):
                        mm(o, H("eq", 16 * w + 8 * h + j), H("rb", 8 * h + j, 8), False, j == 7)
            if t < RO - 1:
                mm(S("pb7", 368, 384), S("cntw"), S("brm"), True, True)
            act(S("tot"), S("pb7", 304, 336), AF.Copy)
            if t < RO - 1:
                act(S("cj"), S("pb7", 368, 384), AF.Identity, total=S("cn"))
            stage[0] = "lo"
            tt(S("lose"), gat(S("tot"), S("o32")), S("thm"), ALU.is_ge)
            for h in HALVES:
                for w in range(2):
                    o = H("pb7", 2 * w + h, 8, 336)
                    mm(o, H("lose", 2 * h + w), H("dhi", h, 8), True, False)
                    mm(o, H("lose", 2 * h + w), S("dlo"), False, True)
            tt(S("off"), S("pb7", 336, 368), S("gf"), ALU.max)
            cp(S("off16"), S("off"))
            if t < RO - 1:
                stage[0] = "cn"
                cp(S("cni"), S("cn"))
                ts(S("cnj"), S("cni"), 15, ALU.bitwise_and)
                ts(S("scol"), S("cnj"), S("thf", t + 1, t + 2), ALU.add, -1.0, ALU.mult)

        def near(h):
            bank, kb = "pb%d" % (2 + h), keyb[h]
            stage[0] = "zc%d" % h
            mm(S(bank, 0, 256), S("oneb"), S("c121"), True, False)
            for i, d in enumerate("zp"):
                for e in range(2):
                    mm(H(bank, 2 * e + i, 64), D(d, 128 * h, 128 * h + 128, 1, e), S("bon"))
            for d in "wzp":
                dist("c", d, h, d == "p")
            stage[0] = "q%d" % h
            mm(S(kb, 0, 256), S("oneb"), S("cr4"), True, False)
            for i, d in enumerate("yx"):
                mm(H(kb, i), H("cf", h), S("qf"))
                mm(H(kb, i), H("eq" + d, h), S("qbp"))
            stage[0] = "n%d" % h
            act(H("dc", h, 256), S(bank, 0, 256), AF.Copy)
            for i in range(4):
                mm(S(kb, i % 2, 256, 2), H("pm", i), H("dc", 2 * h + i // 2), False, i == 3)

        def last(h):
            bank = "pb%d" % (2 + h)
            stage[0] = "n%d" % h
            scan(H("ss", h, 256), S("rsmin"), S(keyb[h], 0, 256), 0.0, ALU.add, ALU.min)
            tt(H("vi", h, 16), S("ss", 256 * h + 15, 256 * h + 256, 16), H("fb", h, 16), ALU.min)
            ts(H("vj", h, 16), H("vi", h, 16), 8191, ALU.bitwise_and)
            cp(H("vf", h, 16), H("vj", h, 16))
            stage[0] = "x%d" % h
            tt(H("xs", h), gat(S("vj", 16 * h, 16 * h + 8), o8), S("d256", 0, 128), ALU.mult)
            mm(H("pb7", h, 8, 384), H("xs", h), S("indf"), True, True)
            xn = H("sxl%d" % t, h, 8)
            act(xn, H("pb7", h, 8, 384), AF.Copy)
            to = (rank + 1) % len(T.cores)
            if t < RO - 1:
                send(xn, H("xl%d" % (t + 1), h, 8), to, "ar%dl%d" % (t + 1, h))
            stage[0] = "w%d" % h
            if h == first:
                act(H("ex", h, 256), gat(H("vf", h, 16), o16), AF.Copy)
            else:
                for w in range(2):
                    act(H("ex", 2 * h + w), gat(H("vf", 2 * h + w, 8), o8), AF.Copy)
            for w in range(2):
                mm(H(bank, w), H("ex", 2 * h + w), S("ids"), True, True)
            for w in range(2):
                tt(H("mm", 2 * w + h), H(bank, w), H("mask", h), ALU.mult)
            tt(gat(tab, H("off16", h, 8)), H("mm", h), H("anm", h), ALU.max)
            stage[0] = "r%d" % h
            if t < RO - 1:
                act(H("sxr%d" % (t + 1), h), H(bank, 0), AF.Copy, 0.0, K13)
                send(H("sxr%d" % (t + 1), h), H("xr%d" % (t + 1), h), to, "ar%dr%d" % (t + 1, h))
            stage[0] = "v%d" % h
            tt(H("zo", h, 8), xn, H("zc", h, 8), ALU.max)
            cp(H("zo16", h, 8), H("zo", h, 8))
            act(H("zs", h), gat(S("prf", 0, z0 + NL), H("zo16", h, 8)), AF.Copy)
            mm(H(bank, 2), S("idb"), H("zs", h), True, False)
            mm(H(bank, 2), S("idb"), side["z"](h), False, True)
            act(H("zh", h), H(bank, 2), AF.Identity, 127.75, 0.5)
            act(H("sz%d" % t, h), H("zh", h), AF.Identity, -128.0)
            if t < RO - 1:
                send(H("sz%d" % t, h), H("prf", h, 128, z0 + NL), to, "ar%dz%d" % (t + 1, h))

        def writes():
            stage[0] = "ww"
            tt(S("rg"), gat(tab, S("yg16")), S("mask"), ALU.subtract)
            for h in HALVES:
                tt(gat(tab, H("off16", 2 + h, 8)), H("rg", h), H("mm", 2 + h), ALU.max)

        stage[1] = t
        for step in STEPS:
            if step[0] in "abc":
                wgather(step[0], int(step[1]))
            elif len(step) == 1:
                {"h": head, "y": partner, "e": pairs, "l": lowest, "w": writes}[step]()
            else:
                {"k": keys, "p": pick, "n": near, "z": last}[step[0]](int(step[1]))
    stage[0] = "ww"
    home = (rank - RO + 1) % len(T.cores)
    send(S("sxl%d" % (RO - 1)), S("xfin"), home, "ar4l")
    send(S("sz%d" % (RO - 1)), S("zfin"), home, "ar4z")
    dma("s", "st0", T.ypar[:, 0:NV // 2], T.tab[:, 0:NV // 2], [S("tab", 0, NV // 2)], [], 3500)
    dma("a", "st1", T.ypar[:, NV // 2:NV], T.tab[:, NV // 2:NV], [S("tab", NV // 2, NV)], [], 3500)
    dma("s", "st2", T.yrec[:], S("xfin")[0], [S("xfin")], [], 2000)
    dma("s", "st3", T.yz[:], T.zfin[:], [S("zfin")], [], 2000)
    return pre + ops


def depend(ops):
    wr, rd, bank, grp = {}, {}, {}, {}
    for i, x in enumerate(ops):
        x["i"] = i
        d, o = set(), set()
        for nm, m in x["r"]:
            d.update(j for a, j in wr.get(nm, ()) if a & m)
        for nm, m in x["w"]:
            d.update(j for a, j in wr.get(nm, ()) if a & m)
            d.update(j for a, j in rd.get(nm, ()) if a & m)
        for nm in set(r[0] for r in x["r"] + x["w"] if r[0][:2] == "pb"):
            s = bank.setdefault(nm, [None, [], []])
            if s[0] != x["e"]:
                s[0], s[1], s[2] = x["e"], [], s[1]
            s[1].append(i)
            d.update(s[2])
        if x["e"] == "p":
            d = set(j for j in d if ops[j]["e"] != "p")
            s = grp.setdefault(x["w"][0][0], [])
            if x["start"] or x["stop"] or x["late"]:
                o.update(s)
            else:
                o.update(j for j in s if ops[j]["start"] or ops[j]["stop"] or ops[j]["late"])
            if x["start"]:
                del s[:]
            s.append(i)
        if "after" in x:
            o.add(x["after"]["i"])
        for nm, m in x["w"]:
            wr[nm] = [(a & ~m, j) for a, j in wr.get(nm, ()) if a & ~m] + [(m, i)]
            rd[nm] = [(a & ~m, j) for a, j in rd.get(nm, ()) if a & ~m]
        for nm, m in x["r"]:
            rd.setdefault(nm, []).append((m, i))
        d.discard(i)
        x["d"], x["o"] = d, o


def schedule(ops):
    n = len(ops)

    def gap(j, x):
        y = ops[j]
        if x["e"] == "x":
            return x["lat"] if j in x["o"] else 0.0
        if j not in x["d"]:
            return 0.0
        return y.get("lat", 0.0) * (y["e"] != "x") + (SELF if y["e"] == x["e"] else HOP)
    back = [[(j, gap(j, x)) for j in x["d"] | x["o"]] for x in ops]
    fwd = [[] for _ in ops]
    for i in range(n):
        for j, gp in back[i]:
            fwd[j].append((i, gp))
    tail = [x.get("lat", 0.0) * (x["e"] != "x") for x in ops]

    def run(key, before, after, first):
        left, at, end = [len(b) for b in before], list(first), [0.0] * n
        ready, free, order = {e: [] for e in "vapgsx"}, {e: 0.0 for e in "vapgsx"}, {e: [] for e in "vapgsx"}
        for i in range(n):
            if not left[i]:
                ready[ops[i]["e"]].append(i)
        soon = {e: min([at[i] for i in r] + [1e18]) for e, r in ready.items()}
        for _ in range(n):
            s, e = min((max(free[e], soon[e]), e) for e in ready)
            r = ready[e]
            i = min((key[j], j) for j in r if at[j] <= s)[1]
            top = min((key[j], j) for j in r if at[j] <= s + AHEAD * ops[i]["c"])[1]
            if key[top] < key[i]:
                i = top
            r.remove(i)
            soon[e] = min([at[j] for j in r] + [1e18])
            end[i] = max(free[e], at[i]) + ops[i]["c"]
            if e != "x":
                free[e] = end[i]
            order[e].append(i)
            for k, gp in after[i]:
                at[k] = max(at[k], end[i] + gp)
                left[k] -= 1
                if not left[k]:
                    ready[ops[k]["e"]].append(k)
                    soon[ops[k]["e"]] = min(soon[ops[k]["e"]], at[k])
        return end, order
    key = [x["key"] for x in ops]
    for i in range(n - 1, -1, -1):
        key[i] = min([key[i]] + [key[k] for k, gp in fwd[i]])
    return run(key, back, fwd, [0.0] * n)[1]


def rank_program(g, core, T, topo):
    rank = T.rank_of(core)
    if rank is None:
        return
    ops = build(g, T, rank, topo)
    depend(ops)
    if not ORDER:
        ORDER.update(schedule(ops))
    order = ORDER
    queue = {"v": g.vector, "a": g.scalar, "p": g.tensor, "g": g, "s": g.sync}
    total = {}
    for e in "vapg":
        k = 0
        for i in order[e]:
            if "sem" not in ops[i] and "send" not in ops[i]:
                k += 1
                ops[i]["sem"], ops[i]["n"], ops[i]["inc"] = "q" + e, k, 1
        total["q" + e] = k
    for x in ops:
        if "send" in x:
            total["sent"] = total.get("sent", 0) + x["send"]
        elif "inc" not in x:
            total[x["sem"]] = x["n"]
    seen, pos, todo = {e: {} for e in "vapgs"}, {e: 0 for e in "vapgs"}, sum(len(order[e]) for e in "vapgs")
    for i in order["x"]:
        ops[i]["seen"] = {}
    while todo:
        for e in "vapgs":
            while pos[e] < len(order[e]) and all("seen" in ops[j] for j in ops[order[e][pos[e]]]["d"]):
                x, need = ops[order[e][pos[e]]], {}
                for j in x["d"]:
                    y = ops[j]
                    if y["n"] > need.get(y["sem"], (0, 0))[0]:
                        need[y["sem"]] = (y["n"], j)
                need = {s: v for s, v in need.items() if v[0] > seen[e].get(s, 0)}
                need = {s: v for s, v in need.items() if not any(ops[w[1]]["seen"].get(s, 0) >= v[0] for u, w in need.items() if u != s)}
                x["waits"] = sorted((s, v[0]) for s, v in need.items())
                for s, v in need.items():
                    seen[e][s] = v[0]
                    for u, k in ops[v[1]]["seen"].items():
                        seen[e][u] = max(seen[e].get(u, 0), k)
                x["seen"] = dict(seen[e])
                pos[e] += 1
                todo -= 1
    for e in "vapgs":
        for i in order[e]:
            x = ops[i]
            for s, k in x["waits"]:
                queue[e].wait_ge(T.sem[s], k)
            ins = x["f"]()
            if "send" not in x:
                ins.then_inc(T.sem[x["sem"]], x.get("inc", 16))
    for s in sorted(total):
        g.wait_ge(T.sem[s], total[s])
